import numpy as np
import ml_dtypes


def mxq(x, axis, fmt="e4m3"):
    dtype, down = {"e4m3": (ml_dtypes.float8_e4m3fn, 7), "e5m2": (ml_dtypes.float8_e5m2, 14)}[fmt]
    v = np.moveaxis(np.asarray(x, np.float32).astype(ml_dtypes.bfloat16).astype(np.float64), axis, -1)
    blocks = v.reshape(v.shape[:-1] + (-1, 32))
    amax = np.abs(blocks).max(-1, keepdims=True)
    byte = np.maximum(np.where(amax > 0, np.frexp(amax)[1] - 1 + 127, 0) - down, 1)
    scale = np.exp2(byte - 127.0)
    codes = (blocks / scale).astype(np.float32).astype(dtype).astype(np.float64)
    return np.moveaxis((codes * scale).reshape(v.shape), -1, axis)


WIDE = False


def mx_kscale(k):
    if not WIDE:
        return np.ones(k)
    levels = np.array([10, -10, 5, -5, 0])
    if k % 512:
        return np.exp2(np.random.permutation(np.resize(levels, k // 32))).repeat(32)
    a = np.empty((k // 512, 16))
    for p in range(k // 512):
        a[p, :8] = np.random.permutation(np.resize(levels, 8))
        for g in range(8):
            far = levels[np.abs(levels - a[p, g]) >= 10]
            a[p, g + 8] = far[np.random.randint(len(far))]
    return np.exp2(a.ravel()).repeat(32)


BF16 = ml_dtypes.bfloat16


def bf(x):
    return np.asarray(x, np.float32).astype(BF16)


def f64(x):
    return np.asarray(x).astype(np.float64)


M, L, D, C, F = 2048, 1024, 1024, 512, 512

SCORE_STD = 1.5
VALUE_STD = 3.0


def draw0():
    s, t, u = mx_kscale(D), mx_kscale(L), mx_kscale(M)
    return {"q": bf(np.random.standard_normal((M, D)) * s),
            "k": bf(np.random.standard_normal((L, D)) * SCORE_STD / np.sqrt(D) / s),
            "latent_bias": bf(0.5 * np.random.standard_normal(L)),
            "latent_gate": bf((1 + 0.1 * np.random.standard_normal(L)) * t),
            "query_gate": bf((1 + 0.1 * np.random.standard_normal(M)) * u),
            "v": bf(np.random.standard_normal((L, C)) * VALUE_STD / t[:, None]),
            "x": bf(np.random.standard_normal((M, F)) * VALUE_STD / u[:, None]),
            "read_gain": bf((1 + 0.1 * np.random.standard_normal(M)) / u),
            "write_gain": bf((1 + 0.1 * np.random.standard_normal(L)) / t)}


def softmax_rows(z):
    e = np.exp(z - z.max(axis=1, keepdims=True))
    return e / e.sum(axis=1, keepdims=True)


def core(q, k, latent_bias, latent_gate, query_gate, v, x, read_gain, write_gain):
    scores = mxq(f64(q), 1, "e4m3") @ mxq(f64(k), 1, "e4m3").T
    p = softmax_rows(scores + f64(latent_bias)[None, :])
    mass = p.sum(axis=0)
    a = p * f64(latent_gate)[None, :] * f64(query_gate)[:, None]
    read = mxq(a, 1, "e4m3") @ mxq(f64(v), 0, "e4m3")
    read = read * f64(read_gain)[:, None]
    written = mxq(a, 0, "e4m3").T @ mxq(f64(x), 0, "e4m3")
    written = written * (f64(write_gain) / mass)[:, None]
    return read, written


def e4m3fn_bytes(y):
    return np.clip(np.asarray(y, np.float64), -448.0, 448.0).astype(np.float32).astype(ml_dtypes.float8_e4m3fn).view(np.uint8)


def e4m3fn_values(b):
    return np.asarray(b, np.uint8).view(ml_dtypes.float8_e4m3fn).astype(np.float64)


def setup_inputs():
    d = draw0()
    x0 = np.asarray(d['q']).astype(np.float64)
    s = (np.max(np.abs(x0), axis=(0,), keepdims=True) / 448.0).astype(np.float32)
    out = {}
    for k, v in d.items():
        if k == 'q':
            out['q_bytes'] = e4m3fn_bytes(x0 / s.astype(np.float64))
            out['q_scale'] = s
        else:
            out[k] = v
    return out


def reference(q_bytes, q_scale, k, latent_bias, latent_gate, query_gate, v, x, read_gain, write_gain):
    return core(e4m3fn_values(q_bytes) * q_scale.astype(np.float64), k, latent_bias, latent_gate, query_gate, v, x, read_gain, write_gain)

@@ -1,0 +1,440 @@
+from contextlib import ExitStack
+
+import concourse.mybir as mybir
+from concourse.masks import make_identity
+
+M, L, D, C, F = 2048, 1024, 1024, 512, 512
+FLOPS = 2 * (M * L * D + M * L * C + M * L * F)
+
+F32 = mybir.dt.float32
+BF16 = mybir.dt.bfloat16
+U32 = mybir.dt.uint32
+U8 = mybir.dt.uint8
+FP8 = mybir.dt.float8_e4m3fn
+FP8X4 = mybir.dt.float8_e4m3fn_x4
+ALU = mybir.AluOpType
+ACT = mybir.ActivationFunctionType
+X = mybir.AxisListType.X
+
+P = 128
+T4 = 4
+G = M // (P * T4)
+NT = M // P
+NB = L // P
+
+
+def tile_perceiver_latent_read_f6_kernel(
+    tc, q_bytes, q_scale, k, latent_bias, latent_gate, query_gate, v, x, read_gain, write_gain, out_0, out_1
+):
+    nc = tc.nc
+    q_view = q_bytes.rearrange("(g p t) d -> g p (t d)", p=P, t=T4)
+    k_view = k.rearrange("(b p) d -> p b d", p=P)
+    v_view = v.rearrange("(c p t) w -> c p (t w)", p=P, t=T4)
+    x_view = x.rearrange("(g p t) w -> g p (t w)", p=P, t=T4)
+    out0_view = out_0.rearrange("(g p t) w -> g t p w", p=P, t=T4)
+    out1_view = out_1.rearrange("(b p) w -> b p w", p=P)
+
+    with ExitStack() as ctx:
+        keep = ctx.enter_context(tc.tile_pool(name="keep", bufs=1))
+        work = ctx.enter_context(tc.tile_pool(name="work", bufs=2))
+        psum = ctx.enter_context(tc.psum_pool(name="psum", bufs=1))
+        ctx.enter_context(tc.manual_schedule())
+
+        scale_bc = keep.tile([P, D], F32, name="scale_bc")
+        bias_bc = keep.tile([P, L], BF16, name="bias_bc")
+        gate_bc = keep.tile([P, L], BF16, name="gate_bc")
+        q_raw = [keep.tile([P, T4 * D], U8, name="q_raw%d" % g, tag="q_raw%d" % g) for g in range(G)]
+        k_raw = [keep.tile([P, 2, D], BF16, name="k_raw%d" % j, tag="k_raw%d" % j) for j in range(4)]
+        v_raw = [keep.tile([P, T4 * C], BF16, name="v_raw%d" % c, tag="v_raw%d" % c) for c in range(2)]
+        x_raw = [keep.tile([P, T4 * F], BF16, name="x_raw%d" % g, tag="x_raw%d" % g) for g in range(G)]
+        qg16 = keep.tile([P, G, T4], BF16, name="qg16")
+        rg16 = keep.tile([P, G, T4], BF16, name="rg16")
+        wg16 = keep.tile([P, P], BF16, name="wg16")
+        qgate = keep.tile([P, G, T4], F32, name="qgate")
+        rgain = keep.tile([P, G, T4], F32, name="rgain")
+        wg32 = keep.tile([P, P], F32, name="wg32")
+        wgain = keep.tile([P, NB], F32, name="wgain")
+        dummy = keep.tile([P, 1], F32, name="dummy")
+        dummy_out = keep.tile([P, 1], F32, name="dummy_out")
+        ident = keep.tile([P, P], F32, name="ident")
+
+        nc.vector.memset(dummy[:], 0.0)
+        nc.scalar.dma_start(out=scale_bc[:], in_=q_scale.rearrange("o d -> (o d)").partition_broadcast(P))
+        nc.scalar.activation(out=dummy_out[:], in_=dummy[:], func=ACT.Exp)
+        nc.sync.dma_start(out=q_raw[0][:], in_=q_view[0])
+        for j in range(4):
+            nc.sync.dma_start(out=k_raw[j][:], in_=k_view[:, 2 * j : 2 * j + 2, :])
+        make_identity(nc, ident[:])
+        nc.gpsimd.memset(wg16[:], 0.0)
+        nc.sync.dma_start(out=bias_bc[:], in_=latent_bias.partition_broadcast(P))
+        for c in range(2):
+            nc.sync.dma_start(out=v_raw[c][:], in_=v_view[c])
+        nc.sync.dma_start(out=gate_bc[:], in_=latent_gate.partition_broadcast(P))
+        nc.sync.dma_start(out=qg16[:], in_=query_gate.rearrange("(g p t) -> p g t", p=P, t=T4))
+        nc.sync.dma_start(out=rg16[:], in_=read_gain.rearrange("(g p t) -> p g t", p=P, t=T4))
+        nc.sync.dma_start(out=wg16[0:NB, :], in_=write_gain.rearrange("(b p) -> b p", p=P))
+        nc.sync.dma_start(out=q_raw[1][:], in_=q_view[1])
+        for g in range(G):
+            nc.sync.dma_start(out=x_raw[g][:], in_=x_view[g])
+            if g < 2:
+                nc.sync.dma_start(out=q_raw[g + 2][:], in_=q_view[g + 2])
+        nc.gpsimd.tensor_copy(out=qgate[:], in_=qg16[:])
+        nc.gpsimd.tensor_copy(out=rgain[:], in_=rg16[:])
+
+        k_codes = [keep.tile([P, 2, 512], U32, name="k_codes%d" % h, tag="k_codes%d" % h, align_bytes=64) for h in range(2)]
+        k_sc = [keep.tile([P, 2, 512], U8, name="k_sc%d" % h, tag="k_sc%d" % h, align_bytes=64) for h in range(2)]
+        v_codes = [keep.tile([P, C], U32, name="v_codes%d" % c, tag="v_codes%d" % c, align_bytes=64) for c in range(2)]
+        v_sc = [keep.tile([P, C], U8, name="v_sc%d" % c, tag="v_sc%d" % c, align_bytes=64) for c in range(2)]
+        x_codes = [keep.tile([P, F], U32, name="x_codes%d" % g, tag="x_codes%d" % g, align_bytes=64) for g in range(G)]
+        x_sc = [keep.tile([P, F], U8, name="x_sc%d" % g, tag="x_sc%d" % g, align_bytes=64) for g in range(G)]
+        am_codes = [keep.tile([P, L], U32, name="am_codes%d" % g, tag="am_codes%d" % g, align_bytes=64) for g in range(G)]
+        am_sc = [keep.tile([P, L], U8, name="am_sc%d" % g, tag="am_sc%d" % g, align_bytes=64) for g in range(G)]
+        mass_ps = psum.tile([P, NT, NB], F32, name="mass_ps", tag="mass", bufs=1)
+
+        k_il = {}
+        v_il = {}
+        x_il = {}
+        q_bf = {}
+        q_il = {}
+        q_codes = {}
+        q_sc = {}
+        bank = {}
+        scores = {}
+        t_neg = {}
+        t_min = {}
+        e_tile = {}
+        e_sum = {}
+        rsum = {}
+        fac = {}
+        a_grp = {}
+        al_il = {}
+        al_codes = {}
+        al_sc = {}
+        read_ps = {}
+        am_il = {}
+        w_ps = {}
+
+        def turn(key, words):
+            ps = psum.tile([P, 4, P], F32, name="turn_ps", tag="turn", bufs=3)
+            bank[key] = ps
+            for c in range(2):
+                for u in range(2):
+                    lo = 256 * c + u
+                    nc.tensor.transpose(ps[:, 2 * c + u, :], words[:, lo : 256 * (c + 1) : 2], ident[:])
+
+        def unload(copy, key, dst):
+            copy(out=dst, in_=bank[key][:].rearrange("p (c u) r -> p c r u", u=2))
+
+        def quant(codes, scales, src):
+            nc.vector.quantize_mx(out=codes.bitcast(FP8X4), scales=scales, in_=src)
+
+        def k_turn(b):
+            turn(("k", b), k_raw[b // 2][:, b % 2, :].bitcast(F32))
+
+        def k_unload(copy, b):
+            h = b // 4
+            if h not in k_il:
+                k_il[h] = work.tile([P, 2, 512, T4], BF16, name="k_il", tag="k_il", bufs=2, align_bytes=64)
+            r0 = P * (b % 4)
+            unload(copy, ("k", b), k_il[h][:].bitcast(F32)[:, :, r0 : r0 + P, :])
+
+        def k_quant(h, c):
+            quant(k_codes[h][:, c, :], k_sc[h][:, c, :], k_il[h][:, c, :, :].rearrange("p l t -> p (l t)"))
+
+        def v_lay(c, h):
+            if h == 0:
+                v_il[c] = work.tile([P, C, T4], BF16, name="v_il", tag="vx_il", bufs=3, align_bytes=64)
+            cols = slice(256 * h, 256 * h + 256)
+            nc.scalar.copy(out=v_il[c][:, cols, :], in_=v_raw[c][:].rearrange("p (t w) -> p w t", t=T4)[:, cols, :])
+
+        def v_quant(c):
+            quant(v_codes[c][:], v_sc[c][:], v_il[c][:].rearrange("p w t -> p (w t)"))
+
+        def x_lay(g, h):
+            if h == 0:
+                x_il[g] = work.tile([P, F, T4], BF16, name="x_il", tag="vx_il", bufs=3, align_bytes=64)
+            cols = slice(256 * h, 256 * h + 256)
+            nc.scalar.copy(out=x_il[g][:, cols, :], in_=x_raw[g][:].rearrange("p (t w) -> p w t", t=T4)[:, cols, :])
+
+        def x_quant(g):
+            quant(x_codes[g][:], x_sc[g][:], x_il[g][:].rearrange("p w t -> p (w t)"))
+
+        def q_widen(i):
+            g, t = divmod(i, T4)
+            q_bf[i] = work.tile([P, D], BF16, name="q_bf", tag="q_bf", bufs=3)
+            nc.vector.tensor_tensor(
+                out=q_bf[i][:], in0=q_raw[g][:, t * D : (t + 1) * D].bitcast(FP8), in1=scale_bc[:], op=ALU.mult
+            )
+
+        def q_turn(i):
+            turn(("q", i), q_bf[i][:].bitcast(F32))
+
+        def q_unload(i):
+            q_il[i] = work.tile([P, 2, P, T4], BF16, name="q_il", tag="q_il", bufs=3, align_bytes=64)
+            unload(nc.scalar.copy, ("q", i), q_il[i][:].bitcast(F32))
+
+        def q_quant(i):
+            q_codes[i] = work.tile([P, 2 * P], U32, name="q_codes", tag="q_codes", bufs=3, align_bytes=64)
+            q_sc[i] = work.tile([P, 2 * P], U8, name="q_sc", tag="q_sc", bufs=3, align_bytes=64)
+            quant(q_codes[i][:], q_sc[i][:], q_il[i][:].rearrange("p c r t -> p (c r t)"))
+
+        def score(i, h):
+            ps = psum.tile([P, 512], F32, name="score_ps", tag="score", bufs=3)
+            scores[i, h] = ps
+            for c in range(2):
+                cols = slice(c * P, (c + 1) * P)
+                nc.tensor.matmul_mx(
+                    out=ps[:],
+                    lhsT=q_codes[i][:, cols].bitcast(FP8X4),
+                    lhsT_scale=q_sc[i][:, cols],
+                    rhs=k_codes[h][:, c, :].bitcast(FP8X4),
+                    rhs_scale=k_sc[h][:, c, :],
+                    start=(c == 0),
+                    stop=(c == 1),
+                )
+
+        def add_bias(i, h):
+            if h == 0:
+                t_neg[i] = work.tile([P, L], F32, name="t_neg", tag="t_neg", bufs=2)
+            cols = slice(512 * h, 512 * h + 512)
+            nc.vector.scalar_tensor_tensor(
+                out=t_neg[i][:, cols], in0=scores[i, h][:], scalar=-1.0, in1=bias_bc[:, cols], op0=ALU.mult, op1=ALU.subtract
+            )
+
+        def row_min(i):
+            t_min[i] = work.tile([P, 1], F32, name="t_min", tag="t_min", bufs=3)
+            nc.vector.tensor_reduce(out=t_min[i][:], in_=t_neg[i][:], axis=X, op=ALU.min)
+
+        def exp(i):
+            e_tile[i] = work.tile([P, L], F32, name="e_tile", tag="e_tile", bufs=4)
+            e_sum[i] = work.tile([P, 1], F32, name="e_sum", tag="e_sum", bufs=3)
+            nc.scalar.activation(
+                out=e_tile[i][:], in_=t_neg[i][:], func=ACT.Exp, bias=t_min[i][:], scale=-1.0, accum_out=e_sum[i][:]
+            )
+
+        def recip(i):
+            g, t = divmod(i, T4)
+            rsum[i] = work.tile([P, 1], F32, name="rsum", tag="rsum", bufs=4)
+            fac[i] = work.tile([P, 1], F32, name="fac", tag="fac", bufs=3)
+            nc.vector.reciprocal(out=rsum[i][:], in_=e_sum[i][:])
+            nc.gpsimd.tensor_tensor(out=fac[i][:], in0=rsum[i][:], in1=qgate[:, g, t : t + 1], op=ALU.mult)
+
+        def gate(i):
+            g, t = divmod(i, T4)
+            if t == 0:
+                a_grp[g] = work.tile([P, T4, L], BF16, name="a_grp", tag="a_grp", bufs=2)
+            nc.vector.scalar_tensor_tensor(
+                out=a_grp[g][:, t, :], in0=e_tile[i][:], scalar=fac[i][:], in1=gate_bc[:], op0=ALU.mult, op1=ALU.mult
+            )
+
+        def mass(i):
+            for b in range(NB):
+                nc.tensor.matmul(
+                    out=mass_ps[:, i, b : b + 1],
+                    lhsT=e_tile[i][:, b * P : (b + 1) * P],
+                    rhs=rsum[i][:],
+                    start=True,
+                    stop=True,
+                )
+
+        def a_turn(i):
+            g, t = divmod(i, T4)
+            turn(("a", i), a_grp[g][:, t, :].bitcast(F32))
+
+        def a_unload(i):
+            al_il[i] = work.tile([P, 2, P, T4], BF16, name="al_il", tag="al_il", bufs=2, align_bytes=64)
+            unload(nc.scalar.copy, ("a", i), al_il[i][:].bitcast(F32))
+
+        def a_quant(i):
+            al_codes[i] = work.tile([P, 2 * P], U32, name="al_codes", tag="al_codes", bufs=3, align_bytes=64)
+            al_sc[i] = work.tile([P, 2 * P], U8, name="al_sc", tag="al_sc", bufs=3, align_bytes=64)
+            quant(al_codes[i][:], al_sc[i][:], al_il[i][:].rearrange("p c r t -> p (c r t)"))
+
+        def read(i):
+            ps = psum.tile([P, C], F32, name="read_ps", tag="read", bufs=1)
+            read_ps[i] = ps
+            for c in range(2):
+                cols = slice(c * P, (c + 1) * P)
+                nc.tensor.matmul_mx(
+                    out=ps[:],
+                    lhsT=al_codes[i][:, cols].bitcast(FP8X4),
+                    lhsT_scale=al_sc[i][:, cols],
+                    rhs=v_codes[c][:].bitcast(FP8X4),
+                    rhs_scale=v_sc[c][:],
+                    start=(c == 0),
+                    stop=(c == 1),
+                )
+
+        def read_out(i):
+            g, t = divmod(i, T4)
+            res = work.tile([P, C], F32, name="read_sb", tag="read_sb", bufs=3)
+            nc.scalar.activation(out=res[:], in_=read_ps[i][:], func=ACT.Copy, scale=rgain[:, g, t : t + 1])
+            nc.sync.dma_start(out=out0_view[g][t], in_=res[:])
+
+        def a_lay(copy, g, c):
+            am_il[g, c] = work.tile([P, 256, T4], BF16, name="am_il", tag="am_il", bufs=4, align_bytes=64)
+            copy(out=am_il[g, c][:], in_=a_grp[g][:].rearrange("p t l -> p l t")[:, 256 * c : 256 * c + 256, :])
+
+        def am_quant(g, c):
+            cols = slice(256 * c, 256 * c + 256)
+            quant(am_codes[g][:, cols], am_sc[g][:, cols], am_il[g, c][:].rearrange("p l t -> p (l t)"))
+
+        def write_passes(b, tag, bufs, groups):
+            if groups[0] == 0:
+                w_ps[b] = psum.tile([P, F], F32, name="write_ps", tag=tag, bufs=bufs)
+            cols = slice(b * P, (b + 1) * P)
+            for g in groups:
+                nc.tensor.matmul_mx(
+                    out=w_ps[b][:],
+                    lhsT=am_codes[g][:, cols].bitcast(FP8X4),
+                    lhsT_scale=am_sc[g][:, cols],
+                    rhs=x_codes[g][:].bitcast(FP8X4),
+                    rhs_scale=x_sc[g][:],
+                    start=(g == 0),
+                    stop=(g == G - 1),
+                )
+
+        def write_out(b, on_scalar, wscale):
+            res = work.tile([P, F], F32, name="write_sb", tag="write_sb", bufs=4)
+            if on_scalar:
+                nc.scalar.activation(out=res[:], in_=w_ps[b][:], func=ACT.Copy, scale=wscale[:, b : b + 1])
+            else:
+                nc.vector.tensor_scalar(out=res[:], in0=w_ps[b][:], scalar1=wscale[:, b : b + 1], scalar2=None, op0=ALU.mult)
+            nc.sync.dma_start(out=out1_view[b], in_=res[:])
+
+        vcopy = nc.vector.tensor_copy
+        scopy = nc.scalar.copy
+        q_widen(0)
+        q_widen(1)
+        k_turn(0)
+        k_turn(1)
+        k_unload(scopy, 0)
+        k_unload(vcopy, 1)
+        k_turn(2)
+        k_turn(3)
+        k_unload(scopy, 2)
+        k_unload(vcopy, 3)
+        q_turn(0)
+        q_unload(0)
+        q_widen(2)
+        k_quant(0, 0)
+        k_quant(0, 1)
+        q_quant(0)
+        k_turn(4)
+        k_turn(5)
+        k_unload(scopy, 4)
+        k_unload(vcopy, 5)
+        k_turn(6)
+        k_turn(7)
+        k_unload(scopy, 6)
+        k_unload(vcopy, 7)
+        q_turn(1)
+        score(0, 0)
+        q_unload(1)
+        q_widen(3)
+        k_quant(1, 0)
+        k_quant(1, 1)
+        q_quant(1)
+        score(0, 1)
+        q_turn(2)
+        q_unload(2)
+
+        lay = {0: [(v_lay, 0, 0), (v_lay, 0, 1)], 1: [(v_lay, 1, 0), (v_lay, 1, 1)]}
+        lay[2] = [(x_lay, 0, 0), (x_lay, 0, 1)]
+        lay[3] = [(x_lay, 1, 0), (x_lay, 1, 1)]
+        lay[4] = [(x_lay, 2, 0), (x_lay, 2, 1)]
+        lay[5] = [(x_lay, 3, 0)]
+        lay[6] = [(x_lay, 3, 1)]
+        late_quant = {1: [(v_quant, 0)], 2: [(v_quant, 1)], 3: [(x_quant, 0)], 4: [(x_quant, 1)], 5: [(x_quant, 2)], 7: [(x_quant, 3)]}
+
+        def has(i):
+            return 0 <= i < NT
+
+        for s in range(NT + 3):
+            if has(s + 3):
+                q_turn(s + 3)
+            if has(s - 2):
+                a_turn(s - 2)
+            if has(s):
+                add_bias(s, 0)
+                add_bias(s, 1)
+            if has(s - 1):
+                recip(s - 1)
+            if has(s + 2):
+                q_quant(s + 2)
+            for job in late_quant.get(s, []):
+                job[0](*job[1:])
+            if has(s + 1):
+                score(s + 1, 0)
+                score(s + 1, 1)
+            if has(s + 3):
+                q_unload(s + 3)
+            if has(s - 2):
+                a_unload(s - 2)
+            for job in lay.get(s, []):
+                job[0](*job[1:])
+            if 5 <= s < 17:
+                gg, cc = divmod(s - 5, T4)
+                a_lay(scopy, gg, cc)
+            if has(s):
+                row_min(s)
+                exp(s)
+            if has(s + 4):
+                q_widen(s + 4)
+            if 6 <= s < 18:
+                gg, cc = divmod(s - 6, T4)
+                am_quant(gg, cc)
+            if s == 17:
+                a_lay(vcopy, 3, 0)
+                a_lay(scopy, 3, 1)
+                a_lay(vcopy, 3, 2)
+            if has(s - 2):
+                a_quant(s - 2)
+            if has(s - 3):
+                read(s - 3)
+                read_out(s - 3)
+            if has(s - 2):
+                mass(s - 2)
+            if has(s - 1):
+                gate(s - 1)
+            if s == 8:
+                scopy(out=wg32[:], in_=wg16[:])
+                ps = psum.tile([P, 4, P], F32, name="turn_ps", tag="turn", bufs=3)
+                nc.tensor.transpose(ps[:, 0, :], wg32[:], ident[:])
+                scopy(out=wgain[:], in_=ps[:, 0, 0:NB])
+            if s == 17:
+                for b in range(3):
+                    write_passes(b, "score", 3, (0, 1, 2))
+                for b in range(3, 5):
+                    write_passes(b, "turn", 3, (0, 1, 2))
+
+        msum = keep.tile([P, NB], F32, name="msum")
+        mrec = keep.tile([P, NB], F32, name="mrec")
+        wscale = keep.tile([P, NB], F32, name="wscale")
+        am_quant(3, 0)
+        a_lay(scopy, 3, 3)
+        am_quant(3, 1)
+        nc.vector.tensor_reduce(out=msum[:], in_=mass_ps[:].rearrange("p i b -> p b i"), axis=X, op=ALU.add)
+        am_quant(3, 2)
+        nc.vector.reciprocal(out=mrec[:], in_=msum[:])
+        am_quant(3, 3)
+        nc.vector.tensor_tensor(out=wscale[:], in0=mrec[:], in1=wgain[:], op=ALU.mult)
+        write_passes(5, "turn", 3, (0, 1, 2))
+        write_passes(0, "score", 3, (3,))
+        write_passes(1, "score", 3, (3,))
+        write_out(0, True, wscale)
+        write_out(1, False, wscale)
+        write_passes(2, "score", 3, (3,))
+        write_passes(3, "turn", 3, (3,))
+        write_out(2, True, wscale)
+        write_out(3, False, wscale)
+        write_passes(6, "mass", 1, (0, 1, 2))
+        write_passes(7, "read", 1, (0, 1, 2))
+        write_passes(4, "turn", 3, (3,))
+        write_passes(5, "turn", 3, (3,))
+        write_out(4, True, wscale)
+        write_out(5, False, wscale)
+        write_passes(6, "mass", 1, (3,))
+        write_passes(7, "read", 1, (3,))
+        write_out(6, True, wscale)
+        write_out(7, False, wscale)

@@ -89,7 +89,12 @@ def tile_perceiver_latent_read_f6_kernel(
         x_sc = [keep.tile([P, F], U8, name="x_sc%d" % g, tag="x_sc%d" % g, align_bytes=64) for g in range(G)]
         am_codes = [keep.tile([P, L], U32, name="am_codes%d" % g, tag="am_codes%d" % g, align_bytes=64) for g in range(G)]
         am_sc = [keep.tile([P, L], U8, name="am_sc%d" % g, tag="am_sc%d" % g, align_bytes=64) for g in range(G)]
-        mass_ps = psum.tile([P, NT, NB], F32, name="mass_ps", tag="mass", bufs=1)
+        mass_ps = psum.tile([P, 512], F32, name="mass_ps", tag="mass", bufs=1)
+        ones = keep.tile([P, 64], F32, name="ones")
+        rz = [keep.tile([P, 192], F32, name="rz%d" % j, tag="rz%d" % j) for j in range(2)]
+        nc.gpsimd.memset(ones[:], 1.0)
+        for j in range(2):
+            nc.gpsimd.memset(rz[j][:], 0.0)
 
         k_il = {}
         v_il = {}
@@ -227,14 +232,18 @@ def tile_perceiver_latent_read_f6_kernel(
                 out=a_grp[g][:, t, :], in0=e_tile[i][:], scalar=fac[i][:], in1=gate_bc[:], op0=ALU.mult, op1=ALU.mult
             )
 
+        def fill(i):
+            nc.scalar.activation(out=rz[i % 2][:, 64:128], in_=ones[:], func=ACT.Copy, scale=rsum[i][:])
+
         def mass(i):
-            for b in range(NB):
+            for h in range(2):
+                lo = 64 * (1 - h)
                 nc.tensor.matmul(
-                    out=mass_ps[:, i, b : b + 1],
-                    lhsT=e_tile[i][:, b * P : (b + 1) * P],
-                    rhs=rsum[i][:],
-                    start=True,
-                    stop=True,
+                    out=mass_ps[:],
+                    lhsT=rz[i % 2][:, lo : lo + P],
+                    rhs=e_tile[i][:, 512 * h : 512 * h + 512],
+                    start=(i == 0 and h == 0),
+                    stop=(i == NT - 1 and h == 1),
                 )
 
         def a_turn(i):
@@ -267,7 +276,7 @@ def tile_perceiver_latent_read_f6_kernel(
 
         def read_out(i):
             g, t = divmod(i, T4)
-            res = work.tile([P, C], F32, name="read_sb", tag="read_sb", bufs=3)
+            res = work.tile([P, C], F32, name="read_sb", tag="read_sb", bufs=4)
             nc.scalar.activation(out=res[:], in_=read_ps[i][:], func=ACT.Copy, scale=rgain[:, g, t : t + 1])
             nc.sync.dma_start(out=out0_view[g][t], in_=res[:])
 
@@ -295,7 +304,7 @@ def tile_perceiver_latent_read_f6_kernel(
                 )
 
         def write_out(b, on_scalar, wscale):
-            res = work.tile([P, F], F32, name="write_sb", tag="write_sb", bufs=4)
+            res = work.tile([P, F], F32, name="write_sb", tag="write_sb", bufs=8)
             if on_scalar:
                 nc.scalar.activation(out=res[:], in_=w_ps[b][:], func=ACT.Copy, scale=wscale[:, b : b + 1])
             else:
@@ -350,14 +359,13 @@ def tile_perceiver_latent_read_f6_kernel(
         def has(i):
             return 0 <= i < NT
 
-        for s in range(NT + 3):
-            if has(s + 3):
-                q_turn(s + 3)
+        for s in range(NT):
             if has(s - 2):
                 a_turn(s - 2)
-            if has(s):
-                add_bias(s, 0)
-                add_bias(s, 1)
+            if has(s + 3):
+                q_turn(s + 3)
+            add_bias(s, 0)
+            add_bias(s, 1)
             if has(s - 1):
                 recip(s - 1)
             if has(s + 2):
@@ -371,30 +379,27 @@ def tile_perceiver_latent_read_f6_kernel(
                 q_unload(s + 3)
             if has(s - 2):
                 a_unload(s - 2)
+            if has(s - 1):
+                fill(s - 1)
             for job in lay.get(s, []):
                 job[0](*job[1:])
-            if 5 <= s < 17:
+            if s >= 5:
                 gg, cc = divmod(s - 5, T4)
                 a_lay(scopy, gg, cc)
-            if has(s):
-                row_min(s)
-                exp(s)
+            row_min(s)
+            exp(s)
             if has(s + 4):
                 q_widen(s + 4)
-            if 6 <= s < 18:
+            if s >= 6:
                 gg, cc = divmod(s - 6, T4)
                 am_quant(gg, cc)
-            if s == 17:
-                a_lay(vcopy, 3, 0)
-                a_lay(scopy, 3, 1)
-                a_lay(vcopy, 3, 2)
             if has(s - 2):
                 a_quant(s - 2)
             if has(s - 3):
                 read(s - 3)
                 read_out(s - 3)
-            if has(s - 2):
-                mass(s - 2)
+            if has(s - 1):
+                mass(s - 1)
             if has(s - 1):
                 gate(s - 1)
             if s == 8:
@@ -402,39 +407,73 @@ def tile_perceiver_latent_read_f6_kernel(
                 ps = psum.tile([P, 4, P], F32, name="turn_ps", tag="turn", bufs=3)
                 nc.tensor.transpose(ps[:, 0, :], wg32[:], ident[:])
                 scopy(out=wgain[:], in_=ps[:, 0, 0:NB])
-            if s == 17:
+            if s == 14:
+                write_passes(3, "turn", 3, (0, 1))
+            if s == 15:
+                write_passes(4, "turn", 3, (0, 1))
                 for b in range(3):
-                    write_passes(b, "score", 3, (0, 1, 2))
-                for b in range(3, 5):
-                    write_passes(b, "turn", 3, (0, 1, 2))
+                    write_passes(b, "score", 3, (0, 1))
 
-        msum = keep.tile([P, NB], F32, name="msum")
-        mrec = keep.tile([P, NB], F32, name="mrec")
-        wscale = keep.tile([P, NB], F32, name="wscale")
+        msum = keep.tile([P, 512], F32, name="msum")
+        mrec = keep.tile([P, 4, 2], F32, name="mrec")
+        wscale = keep.tile([P, 2, 4], F32, name="wscale")
+        a_turn(14)
+        am_quant(2, 2)
+        recip(15)
+        a_unload(14)
+        fill(15)
+        a_lay(scopy, 2, 3)
+        read(13)
+        read_out(13)
+        a_quant(14)
+        gate(15)
+        am_quant(2, 3)
+        for b in range(5):
+            write_passes(b, "", 1, (2,))
+        a_turn(15)
+        mass(15)
+        read(14)
+        a_lay(vcopy, 3, 0)
+        a_lay(scopy, 3, 1)
         am_quant(3, 0)
-        a_lay(scopy, 3, 3)
+        a_lay(vcopy, 3, 2)
+        a_unload(15)
         am_quant(3, 1)
-        nc.vector.tensor_reduce(out=msum[:], in_=mass_ps[:].rearrange("p i b -> p b i"), axis=X, op=ALU.add)
+        scopy(out=msum[:], in_=mass_ps[:])
+        m_ps = psum.tile([P, 4, P], F32, name="turn_ps", tag="turn", bufs=3)
+        for j in range(4):
+            nc.tensor.transpose(m_ps[:, j, :], msum[:, j * P : (j + 1) * P], ident[:])
+        a_quant(15)
         am_quant(3, 2)
-        nc.vector.reciprocal(out=mrec[:], in_=msum[:])
+        a_lay(vcopy, 3, 3)
+        nc.vector.reciprocal(out=mrec[:], in_=m_ps[:, :, 0:P:64])
         am_quant(3, 3)
-        nc.vector.tensor_tensor(out=wscale[:], in0=mrec[:], in1=wgain[:], op=ALU.mult)
+        nc.vector.tensor_tensor(
+            out=wscale[:],
+            in0=mrec[:].rearrange("p j h -> p h j"),
+            in1=wgain[:].rearrange("p (h j) -> p h j", j=4),
+            op=ALU.mult,
+        )
+        ws = wscale[:].rearrange("p h j -> p (h j)")
+        read_out(14)
+        read(15)
+        write_passes(0, "", 1, (3,))
+        write_passes(1, "", 1, (3,))
+        read_out(15)
+        write_out(0, True, ws)
+        write_out(1, False, ws)
+        write_passes(2, "", 1, (3,))
+        write_passes(3, "", 1, (3,))
         write_passes(5, "turn", 3, (0, 1, 2))
-        write_passes(0, "score", 3, (3,))
-        write_passes(1, "score", 3, (3,))
-        write_out(0, True, wscale)
-        write_out(1, False, wscale)
-        write_passes(2, "score", 3, (3,))
-        write_passes(3, "turn", 3, (3,))
-        write_out(2, True, wscale)
-        write_out(3, False, wscale)
+        write_out(2, True, ws)
+        write_out(3, False, ws)
+        write_passes(4, "", 1, (3,))
+        write_passes(5, "", 1, (3,))
         write_passes(6, "mass", 1, (0, 1, 2))
+        write_out(4, True, ws)
+        write_out(5, False, ws)
         write_passes(7, "read", 1, (0, 1, 2))
-        write_passes(4, "turn", 3, (3,))
-        write_passes(5, "turn", 3, (3,))
-        write_out(4, True, wscale)
-        write_out(5, False, wscale)
-        write_passes(6, "mass", 1, (3,))
-        write_passes(7, "read", 1, (3,))
-        write_out(6, True, wscale)
-        write_out(7, False, wscale)
+        write_passes(6, "", 1, (3,))
+        write_passes(7, "", 1, (3,))
+        write_out(6, True, ws)
+        write_out(7, False, ws)

@@ -41,12 +41,15 @@ def tile_perceiver_latent_read_f6_kernel(
         ctx.enter_context(tc.manual_schedule())
 
         scale_bc = keep.tile([P, D], F32, name="scale_bc")
+        srow = work.tile([P, D], F32, name="srow", tag="e_tile", bufs=2)
+        brow = work.tile([P, 2, L], BF16, name="brow", tag="t_neg", bufs=2)
+        ones16 = keep.tile([P, 512], BF16, name="ones16")
+        ones32 = keep.tile([P, P], F32, name="ones32")
         bias_bc = keep.tile([P, L], BF16, name="bias_bc")
         gate_bc = keep.tile([P, L], BF16, name="gate_bc")
         q_raw = [keep.tile([P, T4 * D], U8, name="q_raw%d" % g, tag="q_raw%d" % g) for g in range(G)]
         k_raw = [keep.tile([P, 2, D], BF16, name="k_raw%d" % j, tag="k_raw%d" % j) for j in range(4)]
         v_raw = [keep.tile([P, T4 * C], BF16, name="v_raw%d" % c, tag="v_raw%d" % c) for c in range(2)]
-        x_raw = [keep.tile([P, T4 * F], BF16, name="x_raw%d" % g, tag="x_raw%d" % g) for g in range(G)]
         qg16 = keep.tile([P, G, T4], BF16, name="qg16")
         rg16 = keep.tile([P, G, T4], BF16, name="rg16")
         wg16 = keep.tile([P, P], BF16, name="wg16")
@@ -58,26 +61,31 @@ def tile_perceiver_latent_read_f6_kernel(
         dummy_out = keep.tile([P, 1], F32, name="dummy_out")
         ident = keep.tile([P, P], F32, name="ident")
 
+        nc.vector.memset(srow[:], 0.0)
         nc.vector.memset(dummy[:], 0.0)
-        nc.scalar.dma_start(out=scale_bc[:], in_=q_scale.rearrange("o d -> (o d)").partition_broadcast(P))
+        nc.vector.memset(ones16[:], 1.0)
+        nc.vector.memset(ones32[:], 1.0)
+        nc.scalar.dma_start(out=srow[0:1, :], in_=q_scale)
         nc.scalar.activation(out=dummy_out[:], in_=dummy[:], func=ACT.Exp)
+
+        nc.sync.dma_start(out=k_raw[0][:], in_=k_view[:, 0:2, :])
         nc.sync.dma_start(out=q_raw[0][:], in_=q_view[0])
-        for j in range(4):
+        for j in range(1, 4):
             nc.sync.dma_start(out=k_raw[j][:], in_=k_view[:, 2 * j : 2 * j + 2, :])
         make_identity(nc, ident[:])
+        nc.gpsimd.memset(brow[:], 0.0)
+        nc.gpsimd.dma_start(out=brow[0:1, 0, :], in_=latent_bias.rearrange("(o l) -> o l", o=1))
+        nc.gpsimd.dma_start(out=brow[0:1, 1, :], in_=latent_gate.rearrange("(o l) -> o l", o=1))
         nc.gpsimd.memset(wg16[:], 0.0)
-        nc.sync.dma_start(out=bias_bc[:], in_=latent_bias.partition_broadcast(P))
+        nc.gpsimd.dma_start(out=qg16[:], in_=query_gate.rearrange("(g p t) -> p g t", p=P, t=T4))
+        nc.gpsimd.dma_start(out=rg16[:], in_=read_gain.rearrange("(g p t) -> p g t", p=P, t=T4))
+        nc.gpsimd.dma_start(out=wg16[0:NB, :], in_=write_gain.rearrange("(b p) -> b p", p=P))
+        nc.sync.dma_start(out=q_raw[1][:], in_=q_view[1])
         for c in range(2):
             nc.sync.dma_start(out=v_raw[c][:], in_=v_view[c])
-        nc.sync.dma_start(out=gate_bc[:], in_=latent_gate.partition_broadcast(P))
-        nc.sync.dma_start(out=qg16[:], in_=query_gate.rearrange("(g p t) -> p g t", p=P, t=T4))
-        nc.sync.dma_start(out=rg16[:], in_=read_gain.rearrange("(g p t) -> p g t", p=P, t=T4))
-        nc.sync.dma_start(out=wg16[0:NB, :], in_=write_gain.rearrange("(b p) -> b p", p=P))
-        nc.sync.dma_start(out=q_raw[1][:], in_=q_view[1])
-        for g in range(G):
-            nc.sync.dma_start(out=x_raw[g][:], in_=x_view[g])
-            if g < 2:
-                nc.sync.dma_start(out=q_raw[g + 2][:], in_=q_view[g + 2])
+        x_raw = [keep.tile([P, T4 * F], BF16, name="x_raw%d" % g, tag="k_raw%d" % g) for g in range(G)]
+        late_loads = [(x_raw[0], x_view[0]), (q_raw[2], q_view[2]), (x_raw[1], x_view[1])]
+        late_loads += [(x_raw[2], x_view[2]), (q_raw[3], q_view[3]), (x_raw[3], x_view[3])]
         nc.gpsimd.tensor_copy(out=qgate[:], in_=qg16[:])
         nc.gpsimd.tensor_copy(out=rgain[:], in_=rg16[:])
 
@@ -89,12 +97,7 @@ def tile_perceiver_latent_read_f6_kernel(
         x_sc = [keep.tile([P, F], U8, name="x_sc%d" % g, tag="x_sc%d" % g, align_bytes=64) for g in range(G)]
         am_codes = [keep.tile([P, L], U32, name="am_codes%d" % g, tag="am_codes%d" % g, align_bytes=64) for g in range(G)]
         am_sc = [keep.tile([P, L], U8, name="am_sc%d" % g, tag="am_sc%d" % g, align_bytes=64) for g in range(G)]
-        mass_ps = psum.tile([P, 512], F32, name="mass_ps", tag="mass", bufs=1)
-        ones = keep.tile([P, 64], F32, name="ones")
-        rz = [keep.tile([P, 192], F32, name="rz%d" % j, tag="rz%d" % j) for j in range(2)]
-        nc.gpsimd.memset(ones[:], 1.0)
-        for j in range(2):
-            nc.gpsimd.memset(rz[j][:], 0.0)
+        mass_ps = [psum.tile([P, 4, P], F32, name="mass_ps%d" % j, tag="mass%d" % j, bufs=1) for j in range(2)]
 
         k_il = {}
         v_il = {}
@@ -110,7 +113,7 @@ def tile_perceiver_latent_read_f6_kernel(
         e_tile = {}
         e_sum = {}
         rsum = {}
-        fac = {}
+        p_tile = {}
         a_grp = {}
         al_il = {}
         al_codes = {}
@@ -167,9 +170,14 @@ def tile_perceiver_latent_read_f6_kernel(
         def q_widen(i):
             g, t = divmod(i, T4)
             q_bf[i] = work.tile([P, D], BF16, name="q_bf", tag="q_bf", bufs=3)
-            nc.vector.tensor_tensor(
-                out=q_bf[i][:], in0=q_raw[g][:, t * D : (t + 1) * D].bitcast(FP8), in1=scale_bc[:], op=ALU.mult
-            )
+            pieces = 2 if i == 0 else 1
+            width = D // pieces
+            for j in range(pieces):
+                lo = t * D + j * width
+                cols = slice(j * width, (j + 1) * width)
+                nc.vector.tensor_tensor(
+                    out=q_bf[i][:, cols], in0=q_raw[g][:, lo : lo + width].bitcast(FP8), in1=scale_bc[:, cols], op=ALU.mult
+                )
 
         def q_turn(i):
             turn(("q", i), q_bf[i][:].bitcast(F32))
@@ -184,7 +192,7 @@ def tile_perceiver_latent_read_f6_kernel(
             quant(q_codes[i][:], q_sc[i][:], q_il[i][:].rearrange("p c r t -> p (c r t)"))
 
         def score(i, h):
-            ps = psum.tile([P, 512], F32, name="score_ps", tag="score", bufs=3)
+            ps = psum.tile([P, 512], F32, name="score_ps", tag="score", bufs=2)
             scores[i, h] = ps
             for c in range(2):
                 cols = slice(c * P, (c + 1) * P)
@@ -211,39 +219,37 @@ def tile_perceiver_latent_read_f6_kernel(
             nc.vector.tensor_reduce(out=t_min[i][:], in_=t_neg[i][:], axis=X, op=ALU.min)
 
         def exp(i):
-            e_tile[i] = work.tile([P, L], F32, name="e_tile", tag="e_tile", bufs=4)
+            e_tile[i] = work.tile([P, L], F32, name="e_tile", tag="e_tile", bufs=2)
             e_sum[i] = work.tile([P, 1], F32, name="e_sum", tag="e_sum", bufs=3)
             nc.scalar.activation(
                 out=e_tile[i][:], in_=t_neg[i][:], func=ACT.Exp, bias=t_min[i][:], scale=-1.0, accum_out=e_sum[i][:]
             )
 
         def recip(i):
-            g, t = divmod(i, T4)
             rsum[i] = work.tile([P, 1], F32, name="rsum", tag="rsum", bufs=4)
-            fac[i] = work.tile([P, 1], F32, name="fac", tag="fac", bufs=3)
+            p_tile[i] = work.tile([P, L], F32, name="p_tile", tag="p_tile", bufs=2)
             nc.vector.reciprocal(out=rsum[i][:], in_=e_sum[i][:])
-            nc.gpsimd.tensor_tensor(out=fac[i][:], in0=rsum[i][:], in1=qgate[:, g, t : t + 1], op=ALU.mult)
+            nc.gpsimd.tensor_scalar(
+                out=p_tile[i][:], in0=e_tile[i][:], scalar1=rsum[i][:], scalar2=0.0, op0=ALU.mult, op1=ALU.add
+            )
 
         def gate(i):
             g, t = divmod(i, T4)
             if t == 0:
                 a_grp[g] = work.tile([P, T4, L], BF16, name="a_grp", tag="a_grp", bufs=2)
             nc.vector.scalar_tensor_tensor(
-                out=a_grp[g][:, t, :], in0=e_tile[i][:], scalar=fac[i][:], in1=gate_bc[:], op0=ALU.mult, op1=ALU.mult
+                out=a_grp[g][:, t, :], in0=p_tile[i][:], scalar=qgate[:, g, t : t + 1], in1=gate_bc[:], op0=ALU.mult, op1=ALU.mult
             )
 
-        def fill(i):
-            nc.scalar.activation(out=rz[i % 2][:, 64:128], in_=ones[:], func=ACT.Copy, scale=rsum[i][:])
-
         def mass(i):
-            for h in range(2):
-                lo = 64 * (1 - h)
+            for b in range(NB):
                 nc.tensor.matmul(
-                    out=mass_ps[:],
-                    lhsT=rz[i % 2][:, lo : lo + P],
-                    rhs=e_tile[i][:, 512 * h : 512 * h + 512],
-                    start=(i == 0 and h == 0),
-                    stop=(i == NT - 1 and h == 1),
+                    out=mass_ps[b // 4][:, b % 4, :],
+                    lhsT=p_tile[i][:, b * P : (b + 1) * P],
+                    rhs=ident[:],
+                    is_transpose=True,
+                    start=(i == 0 and b % 4 == 0),
+                    stop=(i == NT - 1 and b % 4 == 3),
                 )
 
         def a_turn(i):
@@ -276,7 +282,7 @@ def tile_perceiver_latent_read_f6_kernel(
 
         def read_out(i):
             g, t = divmod(i, T4)
-            res = work.tile([P, C], F32, name="read_sb", tag="read_sb", bufs=4)
+            res = work.tile([P, C], F32, name="read_sb", tag="out_sb", bufs=8)
             nc.scalar.activation(out=res[:], in_=read_ps[i][:], func=ACT.Copy, scale=rgain[:, g, t : t + 1])
             nc.sync.dma_start(out=out0_view[g][t], in_=res[:])
 
@@ -304,7 +310,7 @@ def tile_perceiver_latent_read_f6_kernel(
                 )
 
         def write_out(b, on_scalar, wscale):
-            res = work.tile([P, F], F32, name="write_sb", tag="write_sb", bufs=8)
+            res = work.tile([P, F], F32, name="write_sb", tag="out_sb", bufs=8)
             if on_scalar:
                 nc.scalar.activation(out=res[:], in_=w_ps[b][:], func=ACT.Copy, scale=wscale[:, b : b + 1])
             else:
@@ -313,18 +319,31 @@ def tile_perceiver_latent_read_f6_kernel(
 
         vcopy = nc.vector.tensor_copy
         scopy = nc.scalar.copy
-        q_widen(0)
-        q_widen(1)
+        def spread(copy, dst, ones, row, h):
+            ps = psum.tile([P, 512], F32, name="score_ps", tag="score", bufs=2)
+            cols = slice(512 * h, 512 * h + 512)
+            nc.tensor.matmul(out=ps[:], lhsT=ones, rhs=row[:, cols], start=True, stop=True)
+            copy(out=dst[:, cols], in_=ps[:])
+
+        warm = psum.tile([P, 512], F32, name="read_ps", tag="read", bufs=1)
+        for j in range(5):
+            nc.tensor.matmul(out=warm[:], lhsT=ones16[:, 0:P], rhs=ones16[:], start=True, stop=True)
+        spread(vcopy, scale_bc, ones32[:], srow, 0)
+        spread(scopy, scale_bc, ones32[:], srow, 1)
         k_turn(0)
         k_turn(1)
         k_unload(scopy, 0)
+        q_widen(0)
         k_unload(vcopy, 1)
         k_turn(2)
         k_turn(3)
+        q_turn(0)
         k_unload(scopy, 2)
         k_unload(vcopy, 3)
-        q_turn(0)
+        q_widen(1)
         q_unload(0)
+        for h in range(2):
+            spread(scopy, bias_bc, ones16[:, 0:P], brow[:, 0, :], h)
         q_widen(2)
         k_quant(0, 0)
         k_quant(0, 1)
@@ -347,6 +366,10 @@ def tile_perceiver_latent_read_f6_kernel(
         score(0, 1)
         q_turn(2)
         q_unload(2)
+        for dst, src in late_loads:
+            nc.sync.dma_start(out=dst[:], in_=src)
+        for h in range(2):
+            spread(scopy, gate_bc, ones16[:, 0:P], brow[:, 1, :], h)
 
         lay = {0: [(v_lay, 0, 0), (v_lay, 0, 1)], 1: [(v_lay, 1, 0), (v_lay, 1, 1)]}
         lay[2] = [(x_lay, 0, 0), (x_lay, 0, 1)]
@@ -368,31 +391,31 @@ def tile_perceiver_latent_read_f6_kernel(
             add_bias(s, 1)
             if has(s - 1):
                 recip(s - 1)
+            row_min(s)
+            if has(s + 1):
+                score(s + 1, 0)
+                score(s + 1, 1)
             if has(s + 2):
                 q_quant(s + 2)
             for job in late_quant.get(s, []):
                 job[0](*job[1:])
-            if has(s + 1):
-                score(s + 1, 0)
-                score(s + 1, 1)
             if has(s + 3):
                 q_unload(s + 3)
             if has(s - 2):
                 a_unload(s - 2)
-            if has(s - 1):
-                fill(s - 1)
-            for job in lay.get(s, []):
-                job[0](*job[1:])
+            jobs = list(lay.get(s, []))
             if s >= 5:
-                gg, cc = divmod(s - 5, T4)
-                a_lay(scopy, gg, cc)
-            row_min(s)
+                jobs = [(a_lay, scopy, (s - 5) // T4, (s - 5) % T4)] + jobs
+            if s < 12:
+                jobs[0][0](*jobs[0][1:])
+                jobs = jobs[1:]
             exp(s)
+            for job in jobs:
+                job[0](*job[1:])
             if has(s + 4):
                 q_widen(s + 4)
             if s >= 6:
-                gg, cc = divmod(s - 6, T4)
-                am_quant(gg, cc)
+                am_quant((s - 6) // T4, (s - 6) % T4)
             if has(s - 2):
                 a_quant(s - 2)
             if has(s - 3):
@@ -400,7 +423,6 @@ def tile_perceiver_latent_read_f6_kernel(
                 read_out(s - 3)
             if has(s - 1):
                 mass(s - 1)
-            if has(s - 1):
                 gate(s - 1)
             if s == 8:
                 scopy(out=wg32[:], in_=wg16[:])
@@ -408,30 +430,30 @@ def tile_perceiver_latent_read_f6_kernel(
                 nc.tensor.transpose(ps[:, 0, :], wg32[:], ident[:])
                 scopy(out=wgain[:], in_=ps[:, 0, 0:NB])
             if s == 14:
-                write_passes(3, "turn", 3, (0, 1))
+                write_passes(2, "turn", 3, (0, 1))
             if s == 15:
-                write_passes(4, "turn", 3, (0, 1))
-                for b in range(3):
-                    write_passes(b, "score", 3, (0, 1))
+                write_passes(3, "turn", 3, (0, 1))
+                for b in range(2):
+                    write_passes(b, "score", 2, (0, 1))
 
-        msum = keep.tile([P, 512], F32, name="msum")
-        mrec = keep.tile([P, 4, 2], F32, name="mrec")
-        wscale = keep.tile([P, 2, 4], F32, name="wscale")
+        msum = keep.tile([P, NB], F32, name="msum")
+        mrec = keep.tile([P, NB], F32, name="mrec")
+        wscale = keep.tile([P, NB], F32, name="wscale")
+        ws = wscale
+        recip(15)
         a_turn(14)
         am_quant(2, 2)
-        recip(15)
         a_unload(14)
-        fill(15)
         a_lay(scopy, 2, 3)
         read(13)
         read_out(13)
-        a_quant(14)
         gate(15)
+        a_quant(14)
         am_quant(2, 3)
-        for b in range(5):
-            write_passes(b, "", 1, (2,))
-        a_turn(15)
         mass(15)
+        a_turn(15)
+        for b in range(4):
+            write_passes(b, "", 1, (2,))
         read(14)
         a_lay(vcopy, 3, 0)
         a_lay(scopy, 3, 1)
@@ -439,41 +461,31 @@ def tile_perceiver_latent_read_f6_kernel(
         a_lay(vcopy, 3, 2)
         a_unload(15)
         am_quant(3, 1)
-        scopy(out=msum[:], in_=mass_ps[:])
-        m_ps = psum.tile([P, 4, P], F32, name="turn_ps", tag="turn", bufs=3)
-        for j in range(4):
-            nc.tensor.transpose(m_ps[:, j, :], msum[:, j * P : (j + 1) * P], ident[:])
         a_quant(15)
-        am_quant(3, 2)
         a_lay(vcopy, 3, 3)
-        nc.vector.reciprocal(out=mrec[:], in_=m_ps[:, :, 0:P:64])
+        am_quant(3, 2)
+        nc.vector.tensor_reduce(out=msum[:, 0:4], in_=mass_ps[0][:], axis=X, op=ALU.add)
         am_quant(3, 3)
-        nc.vector.tensor_tensor(
-            out=wscale[:],
-            in0=mrec[:].rearrange("p j h -> p h j"),
-            in1=wgain[:].rearrange("p (h j) -> p h j", j=4),
-            op=ALU.mult,
-        )
-        ws = wscale[:].rearrange("p h j -> p (h j)")
+        nc.vector.tensor_reduce(out=msum[:, 4:8], in_=mass_ps[1][:], axis=X, op=ALU.add)
+        nc.vector.reciprocal(out=mrec[:], in_=msum[:])
+        nc.vector.tensor_tensor(out=wscale[:], in0=mrec[:], in1=wgain[:], op=ALU.mult)
         read_out(14)
-        read(15)
         write_passes(0, "", 1, (3,))
         write_passes(1, "", 1, (3,))
+        write_passes(4, "turn", 3, (0, 1, 2))
+        read(15)
         read_out(15)
-        write_out(0, True, ws)
-        write_out(1, False, ws)
         write_passes(2, "", 1, (3,))
         write_passes(3, "", 1, (3,))
-        write_passes(5, "turn", 3, (0, 1, 2))
+        write_out(0, True, ws)
+        write_out(1, False, ws)
+        write_passes(4, "", 1, (3,))
+        write_passes(6, "mass0", 1, (0, 1, 2, 3))
         write_out(2, True, ws)
         write_out(3, False, ws)
-        write_passes(4, "", 1, (3,))
-        write_passes(5, "", 1, (3,))
-        write_passes(6, "mass", 1, (0, 1, 2))
+        write_passes(7, "mass1", 1, (0, 1, 2, 3))
+        write_passes(5, "read", 1, (0, 1, 2, 3))
         write_out(4, True, ws)
+        write_out(6, False, ws)
+        write_out(7, True, ws)
         write_out(5, False, ws)
-        write_passes(7, "read", 1, (0, 1, 2))
-        write_passes(6, "", 1, (3,))
-        write_passes(7, "", 1, (3,))
-        write_out(6, True, ws)
-        write_out(7, False, ws)

@@ -41,7 +41,7 @@ def tile_perceiver_latent_read_f6_kernel(
         ctx.enter_context(tc.manual_schedule())
 
         scale_bc = keep.tile([P, D], F32, name="scale_bc")
-        srow = work.tile([P, D], F32, name="srow", tag="e_tile", bufs=2)
+        srow = work.tile([P, D], F32, name="srow", tag="e_tile", bufs=3)
         brow = work.tile([P, 2, L], BF16, name="brow", tag="t_neg", bufs=2)
         ones16 = keep.tile([P, 512], BF16, name="ones16")
         ones32 = keep.tile([P, P], F32, name="ones32")
@@ -60,11 +60,13 @@ def tile_perceiver_latent_read_f6_kernel(
         dummy = keep.tile([P, 1], F32, name="dummy")
         dummy_out = keep.tile([P, 1], F32, name="dummy_out")
         ident = keep.tile([P, P], F32, name="ident")
+        ident16 = keep.tile([P, P], BF16, name="ident16")
 
         nc.vector.memset(srow[:], 0.0)
         nc.vector.memset(dummy[:], 0.0)
         nc.vector.memset(ones16[:], 1.0)
         nc.vector.memset(ones32[:], 1.0)
+        nc.vector.memset(brow[:], 0.0)
         nc.scalar.dma_start(out=srow[0:1, :], in_=q_scale)
         nc.scalar.activation(out=dummy_out[:], in_=dummy[:], func=ACT.Exp)
 
@@ -73,9 +75,9 @@ def tile_perceiver_latent_read_f6_kernel(
         for j in range(1, 4):
             nc.sync.dma_start(out=k_raw[j][:], in_=k_view[:, 2 * j : 2 * j + 2, :])
         make_identity(nc, ident[:])
-        nc.gpsimd.memset(brow[:], 0.0)
-        nc.gpsimd.dma_start(out=brow[0:1, 0, :], in_=latent_bias.rearrange("(o l) -> o l", o=1))
-        nc.gpsimd.dma_start(out=brow[0:1, 1, :], in_=latent_gate.rearrange("(o l) -> o l", o=1))
+        nc.sync.dma_start(out=brow[0:1, 0, :], in_=latent_bias.rearrange("(o l) -> o l", o=1))
+        nc.sync.dma_start(out=brow[0:1, 1, :], in_=latent_gate.rearrange("(o l) -> o l", o=1))
+        nc.gpsimd.tensor_copy(out=ident16[:], in_=ident[:])
         nc.gpsimd.memset(wg16[:], 0.0)
         nc.gpsimd.dma_start(out=qg16[:], in_=query_gate.rearrange("(g p t) -> p g t", p=P, t=T4))
         nc.gpsimd.dma_start(out=rg16[:], in_=read_gain.rearrange("(g p t) -> p g t", p=P, t=T4))
@@ -114,6 +116,7 @@ def tile_perceiver_latent_read_f6_kernel(
         e_sum = {}
         rsum = {}
         p_tile = {}
+        fac = {}
         a_grp = {}
         al_il = {}
         al_codes = {}
@@ -136,6 +139,9 @@ def tile_perceiver_latent_read_f6_kernel(
         def quant(codes, scales, src):
             nc.vector.quantize_mx(out=codes.bitcast(FP8X4), scales=scales, in_=src)
 
+        def interleave(copy, dst, src):
+            copy(out=dst.rearrange("p (c i) t -> p c t i", i=4), in_=src.rearrange("p t (c i) -> p c t i", i=4))
+
         def k_turn(b):
             turn(("k", b), k_raw[b // 2][:, b % 2, :].bitcast(F32))
 
@@ -153,7 +159,7 @@ def tile_perceiver_latent_read_f6_kernel(
             if h == 0:
                 v_il[c] = work.tile([P, C, T4], BF16, name="v_il", tag="vx_il", bufs=3, align_bytes=64)
             cols = slice(256 * h, 256 * h + 256)
-            nc.scalar.copy(out=v_il[c][:, cols, :], in_=v_raw[c][:].rearrange("p (t w) -> p w t", t=T4)[:, cols, :])
+            interleave(nc.scalar.copy, v_il[c][:, cols, :], v_raw[c][:].rearrange("p (t w) -> p t w", t=T4)[:, :, cols])
 
         def v_quant(c):
             quant(v_codes[c][:], v_sc[c][:], v_il[c][:].rearrange("p w t -> p (w t)"))
@@ -162,7 +168,7 @@ def tile_perceiver_latent_read_f6_kernel(
             if h == 0:
                 x_il[g] = work.tile([P, F, T4], BF16, name="x_il", tag="vx_il", bufs=3, align_bytes=64)
             cols = slice(256 * h, 256 * h + 256)
-            nc.scalar.copy(out=x_il[g][:, cols, :], in_=x_raw[g][:].rearrange("p (t w) -> p w t", t=T4)[:, cols, :])
+            interleave(nc.scalar.copy, x_il[g][:, cols, :], x_raw[g][:].rearrange("p (t w) -> p t w", t=T4)[:, :, cols])
 
         def x_quant(g):
             quant(x_codes[g][:], x_sc[g][:], x_il[g][:].rearrange("p w t -> p (w t)"))
@@ -219,26 +225,29 @@ def tile_perceiver_latent_read_f6_kernel(
             nc.vector.tensor_reduce(out=t_min[i][:], in_=t_neg[i][:], axis=X, op=ALU.min)
 
         def exp(i):
-            e_tile[i] = work.tile([P, L], F32, name="e_tile", tag="e_tile", bufs=2)
+            e_tile[i] = work.tile([P, L], F32, name="e_tile", tag="e_tile", bufs=3)
             e_sum[i] = work.tile([P, 1], F32, name="e_sum", tag="e_sum", bufs=3)
             nc.scalar.activation(
                 out=e_tile[i][:], in_=t_neg[i][:], func=ACT.Exp, bias=t_min[i][:], scale=-1.0, accum_out=e_sum[i][:]
             )
 
         def recip(i):
+            g, t = divmod(i, T4)
             rsum[i] = work.tile([P, 1], F32, name="rsum", tag="rsum", bufs=4)
-            p_tile[i] = work.tile([P, L], F32, name="p_tile", tag="p_tile", bufs=2)
+            fac[i] = work.tile([P, 1], F32, name="fac", tag="fac", bufs=3)
             nc.vector.reciprocal(out=rsum[i][:], in_=e_sum[i][:])
-            nc.gpsimd.tensor_scalar(
-                out=p_tile[i][:], in0=e_tile[i][:], scalar1=rsum[i][:], scalar2=0.0, op0=ALU.mult, op1=ALU.add
-            )
+            nc.gpsimd.tensor_tensor(out=fac[i][:], in0=rsum[i][:], in1=qgate[:, g, t : t + 1], op=ALU.mult)
+
+        def normalise(i):
+            p_tile[i] = work.tile([P, L], F32, name="p_tile", tag="p_tile", bufs=2)
+            nc.scalar.activation(out=p_tile[i][:], in_=e_tile[i][:], func=ACT.Copy, scale=rsum[i][:])
 
         def gate(i):
             g, t = divmod(i, T4)
             if t == 0:
                 a_grp[g] = work.tile([P, T4, L], BF16, name="a_grp", tag="a_grp", bufs=2)
             nc.vector.scalar_tensor_tensor(
-                out=a_grp[g][:, t, :], in0=p_tile[i][:], scalar=qgate[:, g, t : t + 1], in1=gate_bc[:], op0=ALU.mult, op1=ALU.mult
+                out=a_grp[g][:, t, :], in0=e_tile[i][:], scalar=fac[i][:], in1=gate_bc[:], op0=ALU.mult, op1=ALU.mult
             )
 
         def mass(i):
@@ -288,7 +297,24 @@ def tile_perceiver_latent_read_f6_kernel(
 
         def a_lay(copy, g, c):
             am_il[g, c] = work.tile([P, 256, T4], BF16, name="am_il", tag="am_il", bufs=4, align_bytes=64)
-            copy(out=am_il[g, c][:], in_=a_grp[g][:].rearrange("p t l -> p l t")[:, 256 * c : 256 * c + 256, :])
+            interleave(copy, am_il[g, c][:], a_grp[g][:, :, 256 * c : 256 * c + 256])
+
+        def a_spread(g, c):
+            ps = psum.tile([P, 256, T4], BF16, name="turn_ps", tag="turn", bufs=3)
+            bank["am", g, c] = ps
+            for h in range(2):
+                lo = 256 * c + 128 * h
+                nc.tensor.matmul(
+                    out=ps[:, 128 * h : 128 * h + 128, :],
+                    lhsT=ident16[:],
+                    rhs=a_grp[g][:, :, lo : lo + 128].rearrange("p t l -> p l t"),
+                    start=True,
+                    stop=True,
+                )
+
+        def a_gather(g, c):
+            am_il[g, c] = work.tile([P, 256, T4], BF16, name="am_il", tag="am_il", bufs=4, align_bytes=64)
+            nc.scalar.copy(out=am_il[g, c][:], in_=bank["am", g, c][:])
 
         def am_quant(g, c):
             cols = slice(256 * c, 256 * c + 256)
@@ -351,11 +377,11 @@ def tile_perceiver_latent_read_f6_kernel(
         k_turn(4)
         k_turn(5)
         k_unload(scopy, 4)
-        k_unload(vcopy, 5)
+        k_unload(scopy, 5)
         k_turn(6)
         k_turn(7)
         k_unload(scopy, 6)
-        k_unload(vcopy, 7)
+        k_unload(scopy, 7)
         q_turn(1)
         score(0, 0)
         q_unload(1)
@@ -372,12 +398,9 @@ def tile_perceiver_latent_read_f6_kernel(
             spread(scopy, gate_bc, ones16[:, 0:P], brow[:, 1, :], h)
 
         lay = {0: [(v_lay, 0, 0), (v_lay, 0, 1)], 1: [(v_lay, 1, 0), (v_lay, 1, 1)]}
-        lay[2] = [(x_lay, 0, 0), (x_lay, 0, 1)]
-        lay[3] = [(x_lay, 1, 0), (x_lay, 1, 1)]
-        lay[4] = [(x_lay, 2, 0), (x_lay, 2, 1)]
-        lay[5] = [(x_lay, 3, 0)]
-        lay[6] = [(x_lay, 3, 1)]
-        late_quant = {1: [(v_quant, 0)], 2: [(v_quant, 1)], 3: [(x_quant, 0)], 4: [(x_quant, 1)], 5: [(x_quant, 2)], 7: [(x_quant, 3)]}
+        for h, s in enumerate((2, 3, 4, 5, 7, 9, 11, 13)):
+            lay[s] = [(x_lay, h // 2, h % 2)]
+        late_quant = {1: [(v_quant, 0)], 2: [(v_quant, 1)], 4: [(x_quant, 0)], 6: [(x_quant, 1)], 10: [(x_quant, 2)], 14: [(x_quant, 3)]}
 
         def has(i):
             return 0 <= i < NT
@@ -387,6 +410,8 @@ def tile_perceiver_latent_read_f6_kernel(
                 a_turn(s - 2)
             if has(s + 3):
                 q_turn(s + 3)
+            if s >= 5:
+                a_spread((s - 5) // T4, (s - 5) % T4)
             add_bias(s, 0)
             add_bias(s, 1)
             if has(s - 1):
@@ -405,10 +430,9 @@ def tile_perceiver_latent_read_f6_kernel(
                 a_unload(s - 2)
             jobs = list(lay.get(s, []))
             if s >= 5:
-                jobs = [(a_lay, scopy, (s - 5) // T4, (s - 5) % T4)] + jobs
-            if s < 12:
-                jobs[0][0](*jobs[0][1:])
-                jobs = jobs[1:]
+                a_gather((s - 5) // T4, (s - 5) % T4)
+            if has(s - 1) and s < 15:
+                normalise(s - 1)
             exp(s)
             for job in jobs:
                 job[0](*job[1:])
@@ -422,7 +446,8 @@ def tile_perceiver_latent_read_f6_kernel(
                 read(s - 3)
                 read_out(s - 3)
             if has(s - 1):
-                mass(s - 1)
+                if s < 15:
+                    mass(s - 1)
                 gate(s - 1)
             if s == 8:
                 scopy(out=wg32[:], in_=wg16[:])
@@ -444,14 +469,18 @@ def tile_perceiver_latent_read_f6_kernel(
         a_turn(14)
         am_quant(2, 2)
         a_unload(14)
-        a_lay(scopy, 2, 3)
+        normalise(14)
+        a_spread(2, 3)
+        a_gather(2, 3)
+        normalise(15)
         read(13)
+        mass(14)
         read_out(13)
         gate(15)
         a_quant(14)
         am_quant(2, 3)
-        mass(15)
         a_turn(15)
+        mass(15)
         for b in range(4):
             write_passes(b, "", 1, (2,))
         read(14)
@@ -460,32 +489,34 @@ def tile_perceiver_latent_read_f6_kernel(
         am_quant(3, 0)
         a_lay(vcopy, 3, 2)
         a_unload(15)
-        am_quant(3, 1)
-        a_quant(15)
-        a_lay(vcopy, 3, 3)
-        am_quant(3, 2)
         nc.vector.tensor_reduce(out=msum[:, 0:4], in_=mass_ps[0][:], axis=X, op=ALU.add)
-        am_quant(3, 3)
         nc.vector.tensor_reduce(out=msum[:, 4:8], in_=mass_ps[1][:], axis=X, op=ALU.add)
+        am_quant(3, 1)
+        a_lay(vcopy, 3, 3)
         nc.vector.reciprocal(out=mrec[:], in_=msum[:])
+        a_quant(15)
         nc.vector.tensor_tensor(out=wscale[:], in0=mrec[:], in1=wgain[:], op=ALU.mult)
+        am_quant(3, 2)
+        am_quant(3, 3)
         read_out(14)
         write_passes(0, "", 1, (3,))
+        write_passes(6, "mass0", 1, (0, 1, 2))
         write_passes(1, "", 1, (3,))
-        write_passes(4, "turn", 3, (0, 1, 2))
-        read(15)
-        read_out(15)
+        write_passes(7, "mass1", 1, (0, 1, 2))
         write_passes(2, "", 1, (3,))
         write_passes(3, "", 1, (3,))
+        write_passes(4, "turn", 3, (0, 1, 2))
+        read(15)
         write_out(0, True, ws)
         write_out(1, False, ws)
         write_passes(4, "", 1, (3,))
-        write_passes(6, "mass0", 1, (0, 1, 2, 3))
         write_out(2, True, ws)
         write_out(3, False, ws)
-        write_passes(7, "mass1", 1, (0, 1, 2, 3))
-        write_passes(5, "read", 1, (0, 1, 2, 3))
-        write_out(4, True, ws)
-        write_out(6, False, ws)
-        write_out(7, True, ws)
-        write_out(5, False, ws)
+        write_passes(6, "", 1, (3,))
+        write_passes(7, "", 1, (3,))
+        read_out(15)
+        write_passes(5, "score", 2, (0, 1, 2, 3))
+        write_out(4, False, ws)
+        write_out(6, True, ws)
+        write_out(7, False, ws)
+        write_out(5, True, ws)

@@ -41,10 +41,8 @@ def tile_perceiver_latent_read_f6_kernel(
         ctx.enter_context(tc.manual_schedule())
 
         scale_bc = keep.tile([P, D], F32, name="scale_bc")
-        srow = work.tile([P, D], F32, name="srow", tag="e_tile", bufs=3)
         brow = work.tile([P, 2, L], BF16, name="brow", tag="t_neg", bufs=2)
         ones16 = keep.tile([P, 512], BF16, name="ones16")
-        ones32 = keep.tile([P, P], F32, name="ones32")
         bias_bc = keep.tile([P, L], BF16, name="bias_bc")
         gate_bc = keep.tile([P, L], BF16, name="gate_bc")
         q_raw = [keep.tile([P, T4 * D], U8, name="q_raw%d" % g, tag="q_raw%d" % g) for g in range(G)]
@@ -62,17 +60,14 @@ def tile_perceiver_latent_read_f6_kernel(
         ident = keep.tile([P, P], F32, name="ident")
         ident16 = keep.tile([P, P], BF16, name="ident16")
 
-        nc.vector.memset(srow[:], 0.0)
         nc.vector.memset(dummy[:], 0.0)
         nc.vector.memset(ones16[:], 1.0)
-        nc.vector.memset(ones32[:], 1.0)
         nc.vector.memset(brow[:], 0.0)
-        nc.scalar.dma_start(out=srow[0:1, :], in_=q_scale)
+        nc.scalar.dma_start(out=scale_bc[:], in_=q_scale.rearrange("o d -> (o d)").partition_broadcast(P))
         nc.scalar.activation(out=dummy_out[:], in_=dummy[:], func=ACT.Exp)
 
-        nc.sync.dma_start(out=k_raw[0][:], in_=k_view[:, 0:2, :])
         nc.sync.dma_start(out=q_raw[0][:], in_=q_view[0])
-        for j in range(1, 4):
+        for j in range(4):
             nc.sync.dma_start(out=k_raw[j][:], in_=k_view[:, 2 * j : 2 * j + 2, :])
         make_identity(nc, ident[:])
         nc.sync.dma_start(out=brow[0:1, 0, :], in_=latent_bias.rearrange("(o l) -> o l", o=1))
@@ -176,14 +171,9 @@ def tile_perceiver_latent_read_f6_kernel(
         def q_widen(i):
             g, t = divmod(i, T4)
             q_bf[i] = work.tile([P, D], BF16, name="q_bf", tag="q_bf", bufs=3)
-            pieces = 2 if i == 0 else 1
-            width = D // pieces
-            for j in range(pieces):
-                lo = t * D + j * width
-                cols = slice(j * width, (j + 1) * width)
-                nc.vector.tensor_tensor(
-                    out=q_bf[i][:, cols], in0=q_raw[g][:, lo : lo + width].bitcast(FP8), in1=scale_bc[:, cols], op=ALU.mult
-                )
+            nc.vector.tensor_tensor(
+                out=q_bf[i][:], in0=q_raw[g][:, t * D : (t + 1) * D].bitcast(FP8), in1=scale_bc[:], op=ALU.mult
+            )
 
         def q_turn(i):
             turn(("q", i), q_bf[i][:].bitcast(F32))
@@ -232,11 +222,13 @@ def tile_perceiver_latent_read_f6_kernel(
             )
 
         def recip(i):
-            g, t = divmod(i, T4)
             rsum[i] = work.tile([P, 1], F32, name="rsum", tag="rsum", bufs=4)
-            fac[i] = work.tile([P, 1], F32, name="fac", tag="fac", bufs=3)
             nc.vector.reciprocal(out=rsum[i][:], in_=e_sum[i][:])
-            nc.gpsimd.tensor_tensor(out=fac[i][:], in0=rsum[i][:], in1=qgate[:, g, t : t + 1], op=ALU.mult)
+
+        def factor(i):
+            g, t = divmod(i, T4)
+            fac[i] = work.tile([P, 1], F32, name="fac", tag="fac", bufs=3)
+            nc.scalar.activation(out=fac[i][:], in_=rsum[i][:], func=ACT.Copy, scale=qgate[:, g, t : t + 1])
 
         def normalise(i):
             p_tile[i] = work.tile([P, L], F32, name="p_tile", tag="p_tile", bufs=2)
@@ -351,26 +343,19 @@ def tile_perceiver_latent_read_f6_kernel(
             nc.tensor.matmul(out=ps[:], lhsT=ones, rhs=row[:, cols], start=True, stop=True)
             copy(out=dst[:, cols], in_=ps[:])
 
-        warm = psum.tile([P, 512], F32, name="read_ps", tag="read", bufs=1)
-        for j in range(5):
-            nc.tensor.matmul(out=warm[:], lhsT=ones16[:, 0:P], rhs=ones16[:], start=True, stop=True)
-        spread(vcopy, scale_bc, ones32[:], srow, 0)
-        spread(scopy, scale_bc, ones32[:], srow, 1)
         k_turn(0)
         k_turn(1)
         k_unload(scopy, 0)
         q_widen(0)
+        q_widen(1)
+        q_widen(2)
         k_unload(vcopy, 1)
         k_turn(2)
         k_turn(3)
         q_turn(0)
         k_unload(scopy, 2)
         k_unload(vcopy, 3)
-        q_widen(1)
         q_unload(0)
-        for h in range(2):
-            spread(scopy, bias_bc, ones16[:, 0:P], brow[:, 0, :], h)
-        q_widen(2)
         k_quant(0, 0)
         k_quant(0, 1)
         q_quant(0)
@@ -385,6 +370,8 @@ def tile_perceiver_latent_read_f6_kernel(
         q_turn(1)
         score(0, 0)
         q_unload(1)
+        for h in range(2):
+            spread(scopy, bias_bc, ones16[:, 0:P], brow[:, 0, :], h)
         q_widen(3)
         k_quant(1, 0)
         k_quant(1, 1)
@@ -408,46 +395,49 @@ def tile_perceiver_latent_read_f6_kernel(
         for s in range(NT):
             if has(s - 2):
                 a_turn(s - 2)
-            if has(s + 3):
-                q_turn(s + 3)
-            if s >= 5:
-                a_spread((s - 5) // T4, (s - 5) % T4)
             add_bias(s, 0)
             add_bias(s, 1)
-            if has(s - 1):
-                recip(s - 1)
-            row_min(s)
             if has(s + 1):
                 score(s + 1, 0)
+            if has(s + 3):
+                q_turn(s + 3)
+            if has(s + 1):
                 score(s + 1, 1)
+            if s >= 5:
+                a_spread((s - 5) // T4, (s - 5) % T4)
+            if has(s - 1):
+                recip(s - 1)
             if has(s + 2):
                 q_quant(s + 2)
-            for job in late_quant.get(s, []):
-                job[0](*job[1:])
-            if has(s + 3):
-                q_unload(s + 3)
+            row_min(s)
+            if has(s - 3):
+                read_out(s - 3)
             if has(s - 2):
                 a_unload(s - 2)
-            jobs = list(lay.get(s, []))
+            if has(s - 1):
+                factor(s - 1)
+                if s < 15:
+                    normalise(s - 1)
+            if has(s + 3):
+                q_unload(s + 3)
+            exp(s)
             if s >= 5:
                 a_gather((s - 5) // T4, (s - 5) % T4)
-            if has(s - 1) and s < 15:
-                normalise(s - 1)
-            exp(s)
-            for job in jobs:
+            for job in lay.get(s, []):
                 job[0](*job[1:])
             if has(s + 4):
                 q_widen(s + 4)
+            for job in late_quant.get(s, []):
+                job[0](*job[1:])
             if s >= 6:
                 am_quant((s - 6) // T4, (s - 6) % T4)
             if has(s - 2):
                 a_quant(s - 2)
-            if has(s - 3):
-                read(s - 3)
-                read_out(s - 3)
+            if has(s - 1) and s < 15:
+                mass(s - 1)
+            if has(s - 2):
+                read(s - 2)
             if has(s - 1):
-                if s < 15:
-                    mass(s - 1)
                 gate(s - 1)
             if s == 8:
                 scopy(out=wg32[:], in_=wg16[:])
@@ -466,6 +456,7 @@ def tile_perceiver_latent_read_f6_kernel(
         wscale = keep.tile([P, NB], F32, name="wscale")
         ws = wscale
         recip(15)
+        factor(15)
         a_turn(14)
         am_quant(2, 2)
         a_unload(14)
@@ -473,7 +464,6 @@ def tile_perceiver_latent_read_f6_kernel(
         a_spread(2, 3)
         a_gather(2, 3)
         normalise(15)
-        read(13)
         mass(14)
         read_out(13)
         gate(15)

from contextlib import ExitStack

import concourse.mybir as mybir
from concourse.masks import make_identity

M, L, D, C, F = 2048, 1024, 1024, 512, 512
FLOPS = 2 * (M * L * D + M * L * C + M * L * F)

F32 = mybir.dt.float32
BF16 = mybir.dt.bfloat16
U32 = mybir.dt.uint32
U8 = mybir.dt.uint8
FP8 = mybir.dt.float8_e4m3fn
FP8X4 = mybir.dt.float8_e4m3fn_x4
ALU = mybir.AluOpType
ACT = mybir.ActivationFunctionType
X = mybir.AxisListType.X

P = 128
T4 = 4
G = M // (P * T4)
NT = M // P
NB = L // P


def tile_perceiver_latent_read_f6_kernel(
    tc, q_bytes, q_scale, k, latent_bias, latent_gate, query_gate, v, x, read_gain, write_gain, out_0, out_1
):
    nc = tc.nc
    q_view = q_bytes.rearrange("(g p t) d -> g p (t d)", p=P, t=T4)
    k_view = k.rearrange("(b p) d -> p b d", p=P)
    v_view = v.rearrange("(c p t) w -> c p (t w)", p=P, t=T4)
    x_view = x.rearrange("(g p t) w -> g p (t w)", p=P, t=T4)
    out0_view = out_0.rearrange("(g p t) w -> g t p w", p=P, t=T4)
    out1_view = out_1.rearrange("(b p) w -> b p w", p=P)

    with ExitStack() as ctx:
        keep = ctx.enter_context(tc.tile_pool(name="keep", bufs=1))
        work = ctx.enter_context(tc.tile_pool(name="work", bufs=2))
        psum = ctx.enter_context(tc.psum_pool(name="psum", bufs=1))
        ctx.enter_context(tc.manual_schedule())

        scale_bc = keep.tile([P, D], F32, name="scale_bc")
        brow = work.tile([P, 2, L], BF16, name="brow", tag="t_neg", bufs=2)
        ones16 = keep.tile([P, 512], BF16, name="ones16")
        bias_bc = keep.tile([P, L], BF16, name="bias_bc")
        gate_bc = keep.tile([P, L], BF16, name="gate_bc")
        q_raw = [keep.tile([P, T4 * D], U8, name="q_raw%d" % g, tag="q_raw%d" % g) for g in range(G)]
        k_raw = [keep.tile([P, 2, D], BF16, name="k_raw%d" % j, tag="k_raw%d" % j) for j in range(4)]
        v_raw = [keep.tile([P, T4 * C], BF16, name="v_raw%d" % c, tag="v_raw%d" % c) for c in range(2)]
        qg16 = keep.tile([P, G, T4], BF16, name="qg16")
        rg16 = keep.tile([P, G, T4], BF16, name="rg16")
        wg16 = keep.tile([P, P], BF16, name="wg16")
        qgate = keep.tile([P, G, T4], F32, name="qgate")
        rgain = keep.tile([P, G, T4], F32, name="rgain")
        wg32 = keep.tile([P, P], F32, name="wg32")
        wgain = keep.tile([P, NB], F32, name="wgain")
        dummy = keep.tile([P, 1], F32, name="dummy")
        dummy_out = keep.tile([P, 1], F32, name="dummy_out")
        ident = keep.tile([P, P], F32, name="ident")
        ident16 = keep.tile([P, P], BF16, name="ident16")

        nc.vector.memset(dummy[:], 0.0)
        nc.vector.memset(ones16[:], 1.0)
        nc.vector.memset(brow[:], 0.0)
        nc.scalar.dma_start(out=scale_bc[:], in_=q_scale.rearrange("o d -> (o d)").partition_broadcast(P))
        nc.scalar.activation(out=dummy_out[:], in_=dummy[:], func=ACT.Exp)

        nc.sync.dma_start(out=q_raw[0][:], in_=q_view[0])
        for j in range(4):
            nc.sync.dma_start(out=k_raw[j][:], in_=k_view[:, 2 * j : 2 * j + 2, :])
        make_identity(nc, ident[:])
        nc.sync.dma_start(out=brow[0:1, 0, :], in_=latent_bias.rearrange("(o l) -> o l", o=1))
        nc.sync.dma_start(out=brow[0:1, 1, :], in_=latent_gate.rearrange("(o l) -> o l", o=1))
        nc.gpsimd.tensor_copy(out=ident16[:], in_=ident[:])
        nc.gpsimd.memset(wg16[:], 0.0)
        nc.gpsimd.dma_start(out=qg16[:], in_=query_gate.rearrange("(g p t) -> p g t", p=P, t=T4))
        nc.gpsimd.dma_start(out=rg16[:], in_=read_gain.rearrange("(g p t) -> p g t", p=P, t=T4))
        nc.gpsimd.dma_start(out=wg16[0:NB, :], in_=write_gain.rearrange("(b p) -> b p", p=P))
        nc.sync.dma_start(out=q_raw[1][:], in_=q_view[1])
        for c in range(2):
            nc.sync.dma_start(out=v_raw[c][:], in_=v_view[c])
        x_raw = [keep.tile([P, T4 * F], BF16, name="x_raw%d" % g, tag="k_raw%d" % g) for g in range(G)]
        late_loads = [(x_raw[0], x_view[0]), (q_raw[2], q_view[2]), (x_raw[1], x_view[1])]
        late_loads += [(x_raw[2], x_view[2]), (q_raw[3], q_view[3]), (x_raw[3], x_view[3])]
        nc.gpsimd.tensor_copy(out=qgate[:], in_=qg16[:])
        nc.gpsimd.tensor_copy(out=rgain[:], in_=rg16[:])

        k_codes = [keep.tile([P, 2, 512], U32, name="k_codes%d" % h, tag="k_codes%d" % h, align_bytes=64) for h in range(2)]
        k_sc = [keep.tile([P, 2, 512], U8, name="k_sc%d" % h, tag="k_sc%d" % h, align_bytes=64) for h in range(2)]
        v_codes = [keep.tile([P, C], U32, name="v_codes%d" % c, tag="v_codes%d" % c, align_bytes=64) for c in range(2)]
        v_sc = [keep.tile([P, C], U8, name="v_sc%d" % c, tag="v_sc%d" % c, align_bytes=64) for c in range(2)]
        x_codes = [keep.tile([P, F], U32, name="x_codes%d" % g, tag="x_codes%d" % g, align_bytes=64) for g in range(G)]
        x_sc = [keep.tile([P, F], U8, name="x_sc%d" % g, tag="x_sc%d" % g, align_bytes=64) for g in range(G)]
        am_codes = [keep.tile([P, L], U32, name="am_codes%d" % g, tag="am_codes%d" % g, align_bytes=64) for g in range(G)]
        am_sc = [keep.tile([P, L], U8, name="am_sc%d" % g, tag="am_sc%d" % g, align_bytes=64) for g in range(G)]
        mass_ps = [psum.tile([P, 4, P], F32, name="mass_ps%d" % j, tag="mass%d" % j, bufs=1) for j in range(2)]

        k_il = {}
        v_il = {}
        x_il = {}
        q_bf = {}
        q_il = {}
        q_codes = {}
        q_sc = {}
        bank = {}
        scores = {}
        t_neg = {}
        t_min = {}
        e_tile = {}
        e_sum = {}
        rsum = {}
        p_tile = {}
        fac = {}
        a_grp = {}
        al_il = {}
        al_codes = {}
        al_sc = {}
        read_ps = {}
        am_il = {}
        w_ps = {}

        def turn(key, words):
            ps = psum.tile([P, 4, P], F32, name="turn_ps", tag="turn", bufs=3)
            bank[key] = ps
            for c in range(2):
                for u in range(2):
                    lo = 256 * c + u
                    nc.tensor.transpose(ps[:, 2 * c + u, :], words[:, lo : 256 * (c + 1) : 2], ident[:])

        def unload(copy, key, dst):
            copy(out=dst, in_=bank[key][:].rearrange("p (c u) r -> p c r u", u=2))

        def quant(codes, scales, src):
            nc.vector.quantize_mx(out=codes.bitcast(FP8X4), scales=scales, in_=src)

        def interleave(copy, dst, src):
            copy(out=dst.rearrange("p (c i) t -> p c t i", i=4), in_=src.rearrange("p t (c i) -> p c t i", i=4))

        def k_turn(b):
            turn(("k", b), k_raw[b // 2][:, b % 2, :].bitcast(F32))

        def k_unload(copy, b):
            h = b // 4
            if h not in k_il:
                k_il[h] = work.tile([P, 2, 512, T4], BF16, name="k_il", tag="k_il", bufs=2, align_bytes=64)
            r0 = P * (b % 4)
            unload(copy, ("k", b), k_il[h][:].bitcast(F32)[:, :, r0 : r0 + P, :])

        def k_quant(h, c):
            quant(k_codes[h][:, c, :], k_sc[h][:, c, :], k_il[h][:, c, :, :].rearrange("p l t -> p (l t)"))

        def v_lay(c, h):
            if h == 0:
                v_il[c] = work.tile([P, C, T4], BF16, name="v_il", tag="vx_il", bufs=3, align_bytes=64)
            cols = slice(256 * h, 256 * h + 256)
            interleave(nc.scalar.copy, v_il[c][:, cols, :], v_raw[c][:].rearrange("p (t w) -> p t w", t=T4)[:, :, cols])

        def v_quant(c):
            quant(v_codes[c][:], v_sc[c][:], v_il[c][:].rearrange("p w t -> p (w t)"))

        def x_lay(g, h):
            if h == 0:
                x_il[g] = work.tile([P, F, T4], BF16, name="x_il", tag="vx_il", bufs=3, align_bytes=64)
            cols = slice(256 * h, 256 * h + 256)
            interleave(nc.scalar.copy, x_il[g][:, cols, :], x_raw[g][:].rearrange("p (t w) -> p t w", t=T4)[:, :, cols])

        def x_quant(g):
            quant(x_codes[g][:], x_sc[g][:], x_il[g][:].rearrange("p w t -> p (w t)"))

        def q_widen(i):
            g, t = divmod(i, T4)
            q_bf[i] = work.tile([P, D], BF16, name="q_bf", tag="q_bf", bufs=3)
            nc.vector.tensor_tensor(
                out=q_bf[i][:], in0=q_raw[g][:, t * D : (t + 1) * D].bitcast(FP8), in1=scale_bc[:], op=ALU.mult
            )

        def q_turn(i):
            turn(("q", i), q_bf[i][:].bitcast(F32))

        def q_unload(i):
            q_il[i] = work.tile([P, 2, P, T4], BF16, name="q_il", tag="q_il", bufs=3, align_bytes=64)
            unload(nc.scalar.copy, ("q", i), q_il[i][:].bitcast(F32))

        def q_quant(i):
            q_codes[i] = work.tile([P, 2 * P], U32, name="q_codes", tag="q_codes", bufs=3, align_bytes=64)
            q_sc[i] = work.tile([P, 2 * P], U8, name="q_sc", tag="q_sc", bufs=3, align_bytes=64)
            quant(q_codes[i][:], q_sc[i][:], q_il[i][:].rearrange("p c r t -> p (c r t)"))

        def score(i, h):
            ps = psum.tile([P, 512], F32, name="score_ps", tag="score", bufs=2)
            scores[i, h] = ps
            for c in range(2):
                cols = slice(c * P, (c + 1) * P)
                nc.tensor.matmul_mx(
                    out=ps[:],
                    lhsT=q_codes[i][:, cols].bitcast(FP8X4),
                    lhsT_scale=q_sc[i][:, cols],
                    rhs=k_codes[h][:, c, :].bitcast(FP8X4),
                    rhs_scale=k_sc[h][:, c, :],
                    start=(c == 0),
                    stop=(c == 1),
                )

        def add_bias(i, h):
            if h == 0:
                t_neg[i] = work.tile([P, L], F32, name="t_neg", tag="t_neg", bufs=2)
            cols = slice(512 * h, 512 * h + 512)
            nc.vector.scalar_tensor_tensor(
                out=t_neg[i][:, cols], in0=scores[i, h][:], scalar=-1.0, in1=bias_bc[:, cols], op0=ALU.mult, op1=ALU.subtract
            )

        def row_min(i):
            t_min[i] = work.tile([P, 1], F32, name="t_min", tag="t_min", bufs=3)
            nc.vector.tensor_reduce(out=t_min[i][:], in_=t_neg[i][:], axis=X, op=ALU.min)

        def exp(i):
            e_tile[i] = work.tile([P, L], F32, name="e_tile", tag="e_tile", bufs=3)
            e_sum[i] = work.tile([P, 1], F32, name="e_sum", tag="e_sum", bufs=3)
            nc.scalar.activation(
                out=e_tile[i][:], in_=t_neg[i][:], func=ACT.Exp, bias=t_min[i][:], scale=-1.0, accum_out=e_sum[i][:]
            )

        def recip(i):
            rsum[i] = work.tile([P, 1], F32, name="rsum", tag="rsum", bufs=4)
            nc.vector.reciprocal(out=rsum[i][:], in_=e_sum[i][:])

        def factor(i):
            g, t = divmod(i, T4)
            fac[i] = work.tile([P, 1], F32, name="fac", tag="fac", bufs=3)
            nc.scalar.activation(out=fac[i][:], in_=rsum[i][:], func=ACT.Copy, scale=qgate[:, g, t : t + 1])

        def normalise(i):
            p_tile[i] = work.tile([P, L], F32, name="p_tile", tag="p_tile", bufs=2)
            nc.scalar.activation(out=p_tile[i][:], in_=e_tile[i][:], func=ACT.Copy, scale=rsum[i][:])

        def gate(i):
            g, t = divmod(i, T4)
            if t == 0:
                a_grp[g] = work.tile([P, T4, L], BF16, name="a_grp", tag="a_grp", bufs=2)
            nc.vector.scalar_tensor_tensor(
                out=a_grp[g][:, t, :], in0=e_tile[i][:], scalar=fac[i][:], in1=gate_bc[:], op0=ALU.mult, op1=ALU.mult
            )

        def mass(i):
            for b in range(NB):
                nc.tensor.matmul(
                    out=mass_ps[b // 4][:, b % 4, :],
                    lhsT=p_tile[i][:, b * P : (b + 1) * P],
                    rhs=ident[:],
                    is_transpose=True,
                    start=(i == 0 and b % 4 == 0),
                    stop=(i == NT - 1 and b % 4 == 3),
                )

        def a_turn(i):
            g, t = divmod(i, T4)
            turn(("a", i), a_grp[g][:, t, :].bitcast(F32))

        def a_unload(i):
            al_il[i] = work.tile([P, 2, P, T4], BF16, name="al_il", tag="al_il", bufs=2, align_bytes=64)
            unload(nc.scalar.copy, ("a", i), al_il[i][:].bitcast(F32))

        def a_quant(i):
            al_codes[i] = work.tile([P, 2 * P], U32, name="al_codes", tag="al_codes", bufs=3, align_bytes=64)
            al_sc[i] = work.tile([P, 2 * P], U8, name="al_sc", tag="al_sc", bufs=3, align_bytes=64)
            quant(al_codes[i][:], al_sc[i][:], al_il[i][:].rearrange("p c r t -> p (c r t)"))

        def read(i):
            ps = psum.tile([P, C], F32, name="read_ps", tag="read", bufs=1)
            read_ps[i] = ps
            for c in range(2):
                cols = slice(c * P, (c + 1) * P)
                nc.tensor.matmul_mx(
                    out=ps[:],
                    lhsT=al_codes[i][:, cols].bitcast(FP8X4),
                    lhsT_scale=al_sc[i][:, cols],
                    rhs=v_codes[c][:].bitcast(FP8X4),
                    rhs_scale=v_sc[c][:],
                    start=(c == 0),
                    stop=(c == 1),
                )

        def read_out(i):
            g, t = divmod(i, T4)
            res = work.tile([P, C], F32, name="read_sb", tag="out_sb", bufs=8)
            nc.scalar.activation(out=res[:], in_=read_ps[i][:], func=ACT.Copy, scale=rgain[:, g, t : t + 1])
            nc.sync.dma_start(out=out0_view[g][t], in_=res[:])

        def a_lay(copy, g, c):
            am_il[g, c] = work.tile([P, 256, T4], BF16, name="am_il", tag="am_il", bufs=4, align_bytes=64)
            interleave(copy, am_il[g, c][:], a_grp[g][:, :, 256 * c : 256 * c + 256])

        def a_spread(g, c):
            ps = psum.tile([P, 256, T4], BF16, name="turn_ps", tag="turn", bufs=3)
            bank["am", g, c] = ps
            for h in range(2):
                lo = 256 * c + 128 * h
                nc.tensor.matmul(
                    out=ps[:, 128 * h : 128 * h + 128, :],
                    lhsT=ident16[:],
                    rhs=a_grp[g][:, :, lo : lo + 128].rearrange("p t l -> p l t"),
                    start=True,
                    stop=True,
                )

        def a_gather(g, c):
            am_il[g, c] = work.tile([P, 256, T4], BF16, name="am_il", tag="am_il", bufs=4, align_bytes=64)
            nc.scalar.copy(out=am_il[g, c][:], in_=bank["am", g, c][:])

        def am_quant(g, c):
            cols = slice(256 * c, 256 * c + 256)
            quant(am_codes[g][:, cols], am_sc[g][:, cols], am_il[g, c][:].rearrange("p l t -> p (l t)"))

        def write_passes(b, tag, bufs, groups):
            if groups[0] == 0:
                w_ps[b] = psum.tile([P, F], F32, name="write_ps", tag=tag, bufs=bufs)
            cols = slice(b * P, (b + 1) * P)
            for g in groups:
                nc.tensor.matmul_mx(
                    out=w_ps[b][:],
                    lhsT=am_codes[g][:, cols].bitcast(FP8X4),
                    lhsT_scale=am_sc[g][:, cols],
                    rhs=x_codes[g][:].bitcast(FP8X4),
                    rhs_scale=x_sc[g][:],
                    start=(g == 0),
                    stop=(g == G - 1),
                )

        def write_out(b, on_scalar, wscale):
            res = work.tile([P, F], F32, name="write_sb", tag="out_sb", bufs=8)
            if on_scalar:
                nc.scalar.activation(out=res[:], in_=w_ps[b][:], func=ACT.Copy, scale=wscale[:, b : b + 1])
            else:
                nc.vector.tensor_scalar(out=res[:], in0=w_ps[b][:], scalar1=wscale[:, b : b + 1], scalar2=None, op0=ALU.mult)
            nc.sync.dma_start(out=out1_view[b], in_=res[:])

        vcopy = nc.vector.tensor_copy
        scopy = nc.scalar.copy
        def spread(copy, dst, ones, row, h):
            ps = psum.tile([P, 512], F32, name="score_ps", tag="score", bufs=2)
            cols = slice(512 * h, 512 * h + 512)
            nc.tensor.matmul(out=ps[:], lhsT=ones, rhs=row[:, cols], start=True, stop=True)
            copy(out=dst[:, cols], in_=ps[:])

        k_turn(0)
        k_turn(1)
        k_unload(scopy, 0)
        q_widen(0)
        q_widen(1)
        q_widen(2)
        k_unload(vcopy, 1)
        k_turn(2)
        k_turn(3)
        q_turn(0)
        k_unload(scopy, 2)
        k_unload(vcopy, 3)
        q_unload(0)
        k_quant(0, 0)
        k_quant(0, 1)
        q_quant(0)
        k_turn(4)
        k_turn(5)
        k_unload(scopy, 4)
        k_unload(scopy, 5)
        k_turn(6)
        k_turn(7)
        k_unload(scopy, 6)
        k_unload(scopy, 7)
        q_turn(1)
        score(0, 0)
        q_unload(1)
        for h in range(2):
            spread(scopy, bias_bc, ones16[:, 0:P], brow[:, 0, :], h)
        q_widen(3)
        k_quant(1, 0)
        k_quant(1, 1)
        q_quant(1)
        score(0, 1)
        q_turn(2)
        q_unload(2)
        for dst, src in late_loads:
            nc.sync.dma_start(out=dst[:], in_=src)
        for h in range(2):
            spread(scopy, gate_bc, ones16[:, 0:P], brow[:, 1, :], h)

        lay = {0: [(v_lay, 0, 0), (v_lay, 0, 1)], 1: [(v_lay, 1, 0), (v_lay, 1, 1)]}
        for h, s in enumerate((2, 3, 4, 5, 7, 9, 11, 13)):
            lay[s] = [(x_lay, h // 2, h % 2)]
        late_quant = {1: [(v_quant, 0)], 2: [(v_quant, 1)], 4: [(x_quant, 0)], 6: [(x_quant, 1)], 10: [(x_quant, 2)], 14: [(x_quant, 3)]}

        def has(i):
            return 0 <= i < NT

        for s in range(NT):
            if has(s - 2):
                a_turn(s - 2)
            add_bias(s, 0)
            add_bias(s, 1)
            if has(s + 1):
                score(s + 1, 0)
            if has(s + 3):
                q_turn(s + 3)
            if has(s + 1):
                score(s + 1, 1)
            if s >= 5:
                a_spread((s - 5) // T4, (s - 5) % T4)
            if has(s - 1):
                recip(s - 1)
            if has(s + 2):
                q_quant(s + 2)
            row_min(s)
            if has(s - 3):
                read_out(s - 3)
            if has(s - 2):
                a_unload(s - 2)
            if has(s - 1):
                factor(s - 1)
                if s < 15:
                    normalise(s - 1)
            if has(s + 3):
                q_unload(s + 3)
            exp(s)
            if s >= 5:
                a_gather((s - 5) // T4, (s - 5) % T4)
            for job in lay.get(s, []):
                job[0](*job[1:])
            if has(s + 4):
                q_widen(s + 4)
            for job in late_quant.get(s, []):
                job[0](*job[1:])
            if s >= 6:
                am_quant((s - 6) // T4, (s - 6) % T4)
            if has(s - 2):
                a_quant(s - 2)
            if has(s - 1) and s < 15:
                mass(s - 1)
            if has(s - 2):
                read(s - 2)
            if has(s - 1):
                gate(s - 1)
            if s == 8:
                scopy(out=wg32[:], in_=wg16[:])
                ps = psum.tile([P, 4, P], F32, name="turn_ps", tag="turn", bufs=3)
                nc.tensor.transpose(ps[:, 0, :], wg32[:], ident[:])
                scopy(out=wgain[:], in_=ps[:, 0, 0:NB])
            if s == 14:
                write_passes(2, "turn", 3, (0, 1))
            if s == 15:
                write_passes(3, "turn", 3, (0, 1))
                for b in range(2):
                    write_passes(b, "score", 2, (0, 1))

        msum = keep.tile([P, NB], F32, name="msum")
        mrec = keep.tile([P, NB], F32, name="mrec")
        wscale = keep.tile([P, NB], F32, name="wscale")
        ws = wscale
        recip(15)
        factor(15)
        a_turn(14)
        am_quant(2, 2)
        a_unload(14)
        normalise(14)
        a_spread(2, 3)
        a_gather(2, 3)
        normalise(15)
        mass(14)
        read_out(13)
        gate(15)
        a_quant(14)
        am_quant(2, 3)
        a_turn(15)
        mass(15)
        for b in range(4):
            write_passes(b, "", 1, (2,))
        read(14)
        a_lay(vcopy, 3, 0)
        a_lay(scopy, 3, 1)
        am_quant(3, 0)
        a_lay(vcopy, 3, 2)
        a_unload(15)
        nc.vector.tensor_reduce(out=msum[:, 0:4], in_=mass_ps[0][:], axis=X, op=ALU.add)
        nc.vector.tensor_reduce(out=msum[:, 4:8], in_=mass_ps[1][:], axis=X, op=ALU.add)
        am_quant(3, 1)
        a_lay(vcopy, 3, 3)
        nc.vector.reciprocal(out=mrec[:], in_=msum[:])
        a_quant(15)
        nc.vector.tensor_tensor(out=wscale[:], in0=mrec[:], in1=wgain[:], op=ALU.mult)
        am_quant(3, 2)
        am_quant(3, 3)
        read_out(14)
        write_passes(0, "", 1, (3,))
        write_passes(6, "mass0", 1, (0, 1, 2))
        write_passes(1, "", 1, (3,))
        write_passes(7, "mass1", 1, (0, 1, 2))
        write_passes(2, "", 1, (3,))
        write_passes(3, "", 1, (3,))
        write_passes(4, "turn", 3, (0, 1, 2))
        read(15)
        write_out(0, True, ws)
        write_out(1, False, ws)
        write_passes(4, "", 1, (3,))
        write_out(2, True, ws)
        write_out(3, False, ws)
        write_passes(6, "", 1, (3,))
        write_passes(7, "", 1, (3,))
        read_out(15)
        write_passes(5, "score", 2, (0, 1, 2, 3))
        write_out(4, False, ws)
        write_out(6, True, ws)
        write_out(7, False, ws)
        write_out(5, True, ws)
